import numpy as np, ml_dtypes
CORES = [2,6,10,14,18,22,26,30]
N = 8
import mx_ref
BF = ml_dtypes.bfloat16
def gentries(a):
    return np.ascontiguousarray(a.reshape(8, 16, -1).transpose(0, 2, 1)).reshape(8, -1)
def gtable(e):
    e = np.asarray(e); return np.ascontiguousarray(e.reshape(8, -1, 16).transpose(0, 2, 1)).reshape(128, -1).astype(np.int32)
def gcols(t, e):
    v = np.concatenate([t.reshape(8, 16, -1, 4), np.zeros((8, 16, 1, 4), BF)], axis=2)
    return np.ascontiguousarray(np.stack([v[g][:, e[g]] for g in range(8)])).reshape(128, -1)
def tile(rs):
    return np.stack(rs, axis=2).reshape(128, -1).astype(BF)
def pick(q, e):
    c = np.concatenate([q[0].reshape(128, -1, 4), np.zeros((128, 1, 4), np.uint8)], axis=1); s = np.concatenate([q[1], np.ones((16, 1), np.uint8)], axis=1)
    return (np.ascontiguousarray(c[:, e].reshape(128, -1)), np.ascontiguousarray(s[:, e]))
def join(*qs):
    return (np.concatenate([q[0] for q in qs], axis=1), np.concatenate([q[1] for q in qs], axis=1))
def put(q, e, v):
    c, s = q[0].reshape(128, -1, 4).copy(), q[1].copy(); c[:, e] = v[0].reshape(128, -1, 4); s[:, e] = v[1]
    return (c.reshape(128, -1), s)
def pk(c, s):
    return (np.ascontiguousarray(c), mx_ref.live(s))
def emit(q):
    return q[0], q[1]
def packed(v, rng):
    q = [mx_ref.quantize(np.ascontiguousarray(v[r])) for r in range(N)]
    return np.stack([a for a, b in q]), np.stack([mx_ref.plane(b, rng) for a, b in q])
def values_of_codes():
    e, c = np.zeros((128, 128, 4), np.float32), np.zeros((128, 2, 4), np.uint8)
    e[np.arange(128), np.arange(128), 0] = 1
    c[:127, :, 0] = np.arange(256).reshape(2, 128).T[:127]
    return mx_ref.matmul(mx_ref.quantize(e.reshape(128, 512).astype(BF)), (c.reshape(128, 8), np.full((16, 2), 127, np.uint8))).T.reshape(-1).astype(np.float64)
CODE_VALUE, SCALE_VALUE = values_of_codes(), 2.0 ** (np.arange(256) - 127.0)
def decode(q):
    return (CODE_VALUE[q[0]].reshape(16, 8, -1, 4) * SCALE_VALUE[q[1]][:, None, :, None] + 0.0).reshape(128, -1).astype(np.float32)
def f(rng, *shape):
    return mx_ref.flush((rng.standard_normal(shape, dtype=np.float32) * np.exp2(rng.integers(-2, 3, shape[:-1] + (1,)))).astype(BF))
def wide(rng, *shape, cols=0):
    v = rng.standard_normal(shape, dtype=np.float32) * np.exp2(rng.integers(-12, 13, shape)).astype(np.float32)
    if cols: v *= np.repeat(np.exp2(rng.integers(-cols, cols + 1, shape[:-2] + (1, shape[-1] // 4))) * (rng.random(shape[:-2] + (1, shape[-1] // 4)) > 0.0625), 4, axis=-1).astype(np.float32)
    return mx_ref.flush(v.astype(BF))
C = 352
MASK = [1, 2, 4]
def numbers_of(rng):
    return {"x": np.array(f(rng, N, 128, 4 * C)), "u": np.array(f(rng, N, 128, 512)), "v": np.array(f(rng, N, 128, 512))}
def following(o):
    e = np.zeros_like(o)
    np.put_along_axis(e, o, np.roll(o, -1, axis=-1), axis=-1)
    return e
def rings(rng):
    return following(rng.permuted(np.tile(np.arange(C), (N, 8, 1)), axis=2))
def runs(rng, when, same=False):
    o, go = np.zeros((N, 8, C), np.int64), np.zeros((N, 8, C), bool)
    for r in range(N):
        k = rng.permutation(C)
        for g in range(8):
            p = r ^ MASK[when[g]]
            if p < r: continue
            if not same: k = rng.permutation(C)
            for i, m in ((r, [1, 0, 3, 2]), (p, [2, 0, 3, 1])):
                q = rng.permuted(k.reshape(4, -1), axis=1)[m]
                o[i, g] = np.concatenate([q[:2].T.reshape(-1), q[2:].T.reshape(-1)])
                go[i, g, q[:2].reshape(-1)] = True
    return following(o), go
def stored(e):
    return {"nx": np.stack([gtable(e[r]) for r in range(N)])}
def layers(rng, still=[]):
    w = np.array(f(rng, N, 128, 2048)).reshape(N, 8, 16, 4, 8, 16, 4)
    for i in still:
        w[:, :, i] = 0
        w[:, :, :, :, :, i] = 0
    return w
def weights(rng, w):
    c, s = packed(np.ascontiguousarray(w).reshape(N, 128, 2048), rng)
    return {"wc": c, "ws": s}
def setup_inputs(rng):
    return {**numbers_of(rng), **stored(rings(rng)), **weights(rng, layers(rng))}
def setup_inputs_ties(rng):
    d = numbers_of(rng)
    o = rng.permutation(N)
    k = rng.integers(-1, 2, (N, 8, C)).astype(np.float32)
    k[o[1]] = 1
    x = d["x"].reshape(N, 8, 16, C, 4)
    x[:, :, 0] = 0
    x[:, :, 0, :, 0] = k.astype(BF)
    c = np.ones(N, np.float32)
    c[o[0]] = 0
    c[o[2]] = -1
    u = d["u"].reshape(N, 128, 128, 4)
    u[:, :, ::16] = 0
    for h in range(0, 128, 16): u[:, h, h, 0] = c.astype(BF)
    e, i = rings(rng), np.arange(C)
    for r in range(N):
        p, h = r ^ MASK[0], rng.permutation(8)
        if p < r: continue
        e[p, h[0]] = e[r, h[0]]
        e[p, h[1]] = np.argsort(e[r, h[1]])
        e[r, h[2]], e[p, h[2]] = (i + 1) % C, (i - 1) % C
        e[r, h[3]] = e[p, h[3]] = (i + 1) % C
    w = layers(rng)
    w[:, :, :, :, :, :8] = 0
    return {"x": x.reshape(N, 128, 4 * C), "u": u.reshape(N, 128, 512), "v": d["v"], **stored(e), **weights(rng, w)}
def setup_inputs_near(rng):
    d = numbers_of(rng)
    o = rng.permutation(N) % 4
    k = np.where(o % 2 == 0, 1.0, 2.0 ** -30)
    x = np.zeros((N, 8, 16, C, 4))
    s = rng.integers(-1, 2, (N, 8, C)) * k[:, None, None]
    x[:, :, 0, :, 0] = 1.125 * s
    x[:, :, 1, :, 0] = -1.25 * s
    x[:, :, 8, :, 0] = rng.integers(-1, 2, (N, 8, C)) * 2.0 ** -27
    x[:, :, 8, :, 1] = 2.0 ** -27
    x[:, :, 9:] = (1.0 + rng.integers(0, 128, (N, 8, 7, C, 4)) * 2.0 ** -7) * 2.0 ** -27 * rng.choice([-1.0, 1.0], (N, 8, 7, C, 4))
    w = layers(rng, list(range(9)))
    for r in range(N):
        if o[r] % 2 == 1: x[r, :, 7, :, 0] = 2.0 ** -26
        if o[r] == 3:
            x[r, :, :2] = 0
            x[r, :, 7, :, 0] = 2.0 ** -27
            for g in range(8):
                w[r, g, 8, 0, g, 0, 0] = 2.0 ** -10
                w[r, g, 8, 0, g, 0, 1] = 2.0 ** -8
                w[r, g, 8, 0, g, 1, 0] = -2.0 ** -10
                w[r, g, 8, 0, g, 1, 1] = -1.125 * 2.0 ** -8
        else:
            at = [0, C - 1, int(rng.integers(C)), int(rng.integers(C))]
            for g, j in zip(rng.permutation(8)[:4], at): x[r, g, 0, j, 0] = 2.0 ** 30 * rng.choice([-1.0, 1.0])
    u = d["u"].reshape(N, 128, 128, 4)
    u[:, :, ::16] = 0
    for h in range(0, 128, 16):
        u[:, h, h, 0] = (1.125 * k).astype(np.float32).astype(BF)
        u[:, h + 1, h, 0] = k.astype(np.float32).astype(BF)
    return {"x": x.astype(np.float32).reshape(N, 128, 4 * C).astype(BF), "u": u.reshape(N, 128, 512), "v": d["v"], **stored(rings(rng)), **weights(rng, w)}
def setup_inputs_runs(rng):
    d = numbers_of(rng)
    o = rng.permutation(8)
    when = np.zeros(8, np.int64)
    when[o[4:6]] = 1
    when[o[6:]] = 2
    e, go = runs(rng, when)
    low = -rng.integers(0, 2, (N, 8, C))
    t = np.where(go, 1, low)
    for r in range(N):
        h = rng.permutation(o[:4])
        t[r, h[0]] = 1
        t[r, h[1]] = low[r, h[1]]
    for g in o[4:]:
        for i in range(when[g]): t[:, g] = np.take_along_axis(t[:, g], e[:, g], axis=1)
    x = (1.0 + (2 * rng.integers(0, 64, (N, 16, 8, C, 4)) + 1) * 2.0 ** -7) * np.exp2(-rng.integers(0, 7, (N, 16, 8, C, 4)).astype(np.float64)) * rng.choice([-1.0, 1.0], (N, 16, 8, C, 4))
    c = rng.choice([-1.0, 1.0], (N, 16, 1))
    k = np.exp2(when - 8.0)[:, None]
    x[:, :, 0, :, 0] = np.where(rng.random((N, 16, C)) < 0.5, 1.96875, 1.875) * 2.0 ** 8 * c
    x[:, :, 3, :, 0] = 1.875 * 2.0 ** 7
    x[:, ::2, 1, :, 0] = (8 + t) * k
    x[:, ::2, 2, :, 0] = 8 * k
    u = d["u"].reshape(N, 128, 128, 4)
    u[:, :, ::16] = 0
    for h in range(0, 128, 16):
        u[:, h + 1, h, 0] = 1
        u[:, h + 2, h, 0] = -1
    w = layers(rng, [0, 3, 8, 11])
    for g in range(8):
        for i in (0, 1):
            w[:, g, 8 * i + 3, 0, g, 8 * i, 0] = (64 * c[:, 2 * g + i, 0]).astype(np.float32).astype(BF)
            w[:, g, 8 * i + 3, 0, g, 8 * i + 3, 0] = 32
    for g in o[4:]:
        x[:, 2 * g, 4, :, 0] = -1.0
        x[:, 2 * g, 5, :, 0] = 1.0 - when[g]
        u[:, 16 * g + 4, 16 * g, 0] = 1
        for i in (1, 2, 4, 5): w[:, :, :, :, g, i] = 0
        w[:, g, 4, 0, g, 4, 0] = -32
        w[:, g, 5, 0, g, 4, 0] = 64
        w[:, g, 5, 0, g, 5, 0] = -32
    return {"x": x.astype(np.float32).reshape(N, 128, 4 * C).astype(BF), "u": u.reshape(N, 128, 512), "v": d["v"], **stored(e), **weights(rng, w)}
def setup_inputs_ends(rng):
    d = numbers_of(rng)
    e, go = runs(rng, np.zeros(8, np.int64), True)
    o = rng.permutation(N) % 4
    s = go[:, 0] * 2.0 - 1.0
    small = (1.0 + 0.125 * rng.integers(0, 8, (N, 8, 16, C, 4))) * 2.0 ** -20
    x = (0.9 + 0.1 * rng.random((N, 8, 16, C, 4))) * 2.0 ** 30
    u = d["u"].astype(np.float32).reshape(N, 128, 128, 4)
    v = np.zeros((N, 128, 512), np.float32)
    w = np.zeros((N, 128, 4, 128, 4), np.float32)
    i = np.arange(128)
    for r in range(N):
        if o[r] == 0: x[r] *= s[r][:, None]
        if o[r] == 1: x[r] *= -1
        if o[r] == 2: x[r] *= rng.choice([-1.0, 1.0], (8, 1, C, 1))
        if o[r] == 3: x[r] = small[r] * s[r][:, None]
        x[r, 7, 8:] = small[r, 7, 8:] * rng.choice([-1.0, 1.0], (8, C, 4))
        c = np.array([0.0, 1, 1, 1, -1, -1, -1, -1])[rng.permutation(8)][None, :, None]
        if o[r] < 3: u[r, :, ::16] = c * (0.9 + 0.1 * rng.random((128, 8, 4))) * 2.0 ** 30
        else: u[r, :, ::16] = c * (1.0 + 0.125 * rng.integers(0, 8, (128, 8, 4))) * 2.0 ** -30
        if o[r] < 2: v[r] = (0.9 + 0.1 * rng.random((128, 512))) * 2.0 ** 30
        else: v[r] = (1.0 + 0.125 * rng.integers(0, 8, (128, 512))) * 2.0 ** -30
        v[r] *= rng.choice([-1.0, 1.0], (128, 512))
        k = np.full(128, 32.0)
        if o[r] == 3: k = np.where(i < 120, 2.0 ** -8, 2.0 ** 8)
        for b in range(4): w[r, i, b, i, b] = k
    return {"x": x.astype(np.float32).reshape(N, 128, 4 * C).astype(BF), "u": u.reshape(N, 128, 512).astype(BF), "v": v.astype(BF), **stored(e), **weights(rng, w.astype(BF))}
def setup_inputs_spread(rng):
    d = setup_inputs(rng)
    d["x"] = wide(rng, N, 128, 4 * C, cols=6)
    return d
def check_inputs(d):
    b = []
    for k in ("x", "u", "v"):
        a = np.abs(d[k].astype(np.float32))
        if not (np.isfinite(a).all() and ((a == 0) | (a >= 2.0 ** -30) & (a <= 2.0 ** 30)).all()): b.append("a value of " + k)
    if not ((d["nx"] >= 0) & (d["nx"] < C)).all(): b.append("an entry of nx")
    else:
        e = np.concatenate([gentries(d["nx"][r]) for r in range(N)])
        at, back = np.zeros(8 * N, np.int64), np.zeros(8 * N, np.int64)
        for i in range(1, C + 1):
            at = e[np.arange(8 * N), at]
            back = np.where((at == 0) & (back == 0), i, back)
        if not (back == C).all(): b.append("a ring of nx")
    none, least, most = [emit(mx_ref.quantize(np.full((128, 16), k, np.float32).astype(BF)))[1][0, 0] for k in (0.0, 2.0 ** -8, 2.0 ** 8)]
    for r in range(N):
        if ((d["wc"][r] == 0x7F) | (d["wc"][r] == 0xFF)).any(): b.append("wc: a code that is no number")
        s = mx_ref.live(d["ws"][r])
        if ((s != none) & ((s < least) | (s > most))).any(): b.append("ws: a scale out of range")
    return b
def at(a, e):
    return np.take_along_axis(a, e, axis=1)
def mean(a, b):
    return ((a.astype(np.float32) + b.astype(np.float32)) * np.float32(0.5)).astype(BF)
def reference(x, u, v, nx, wc, ws):
    qu = [mx_ref.quantize(u[r]) for r in range(N)]
    lay = [pk(wc[r], ws[r]) for r in range(N)]
    ring = [gentries(nx[r]).astype(np.int64) for r in range(N)]
    now = [x[r] for r in range(N)]
    for m in MASK:
        t, new, back, z = [], [], [], []
        for r in range(N):
            q = mx_ref.quantize(now[r])
            t.append(decode(q).astype(BF))
            up = mx_ref.matmul(qu[r], q)[::16] > 0
            guest = ring[r ^ m]
            host = np.argsort(guest, axis=1)
            leave = up & ~at(up, host)
            a = ring[r]
            for i in range(8):
                a = np.where(at(leave, a), at(a, a), a)
            new.append(np.where(leave, at(a, host), np.where(at(leave, guest), guest, a)))
            back.append(np.argsort(new[r], axis=1))
            z.append(mx_ref.quantize(mean(gcols(t[r], new[r]), gcols(t[r], back[r]))))
        for r in range(N):
            h = tile([mx_ref.matmul(pick(lay[r], np.arange(128 * b, 128 * b + 128)), z[r ^ m]) * np.float32(0.03125) for b in range(4)])
            now[r] = mean(gcols(t[r], back[r]), gcols(h, new[r]))
        ring = new
    y, nr = np.zeros((N, 128, C), np.float32), np.zeros((N, 8, C), np.float32)
    oc, osc = np.zeros((N, 128, 4 * C), np.uint8), np.zeros((N, 16, C), np.uint8)
    for r in range(N):
        q = mx_ref.quantize(now[r])
        y[r] = mx_ref.matmul(mx_ref.quantize(v[r]), q)
        nr[r] = ring[r]
        oc[r], osc[r] = emit(q)
    return {"y": y, "nr": nr, "oc": oc, "osc": osc}

@@ -1,0 +1,461 @@
+from concourse.bass import DstId, RemoteDMATransfer
+from concourse.mybir import dt, AluOpType, ActivationFunctionType
+
+C = 352
+CH = [(0, 192), (192, 352)]
+MASKS = [1, 2, 4]
+ROUNDS = 3
+W16 = C // 16
+NEG, K = -float(2 ** 22), float(2 ** 20)
+F8 = "float8_e4m3fn_x4"
+
+SCRATCH = {
+    "nxi": ("sbuf", [128, W16], "int32"), "lnxi": ("sbuf", [128, W16], "int32"),
+    "X0": ("sbuf", [128, 4 * C], "bfloat16"), "X1": ("sbuf", [128, 4 * C], "bfloat16"),
+    "ut": ("sbuf", [128, 512], "bfloat16"), "vt": ("sbuf", [128, 512], "bfloat16"),
+    "wq": ("sbuf", [128, 512], F8), "wsq": ("sbuf", [128, 512], "uint8"),
+    "uq": ("sbuf", [128, 128], F8), "uqs": ("sbuf", [128, 128], "uint8"),
+    "up16": ("sbuf", [128, 128], F8), "up16s": ("sbuf", [128, 128], "uint8"),
+    "vq": ("sbuf", [128, 128], F8), "vqs": ("sbuf", [128, 128], "uint8"),
+    "eq": ("sbuf", [128, 512], F8), "eqs": ("sbuf", [128, 512], "uint8"),
+    "zq": ("sbuf", [128, C], F8), "zqs": ("sbuf", [128, C], "uint8"),
+    "EW": ("sbuf", [128, 516], "float32"), "EB": ("sbuf", [128, 516], "bfloat16"),
+    "IOTA": ("sbuf", [128, C], "float32"), "J16": ("sbuf", [128, C], "float32"),
+    "pi": ("sbuf", [128, 1], "int32"), "pj": ("sbuf", [128, 1], "int32"), "p16": ("sbuf", [128, 1], "float32"),
+    "C16": ("sbuf", [128, W16], "float32"), "l16": ("sbuf", [128, W16], "uint16"),
+    "dd": ("sbuf", [128, C], "float32"), "t1": ("sbuf", [128, C], "float32"), "t2": ("sbuf", [128, C], "float32"),
+    "SELD": ("sbuf", [128, C], "bfloat16"), "SELB": ("sbuf", [128, C], "bfloat16"),
+    "off": ("sbuf", [128, 1], "float32"), "thrB": ("sbuf", [128, 1], "float32"),
+    "thr2": ("sbuf", [128, 1], "float32"), "thr3": ("sbuf", [128, 1], "float32"),
+    "jw": ("sbuf", [128, W16], "float32"), "msk": ("sbuf", [128, W16], "float32"),
+    "offj": ("sbuf", [128, W16], "float32"), "offi": ("sbuf", [128, W16], "float32"),
+    "CODD": ("sbuf", [128, C], "float32"), "VC": ("sbuf", [128, C], "float32"), "ONES": ("sbuf", [128, 2 * C], "bfloat16"),
+    "L0f": ("sbuf", [128, W16], "float32"), "La": ("sbuf", [128, W16], "uint16"), "Lb": ("sbuf", [128, W16], "uint16"),
+    "PTa": ("sbuf", [128, C], "float32"), "PTb": ("sbuf", [128, C], "float32"),
+    "Da": ("sbuf", [128, C], "float32"), "Db": ("sbuf", [128, C], "float32"), "DC": ("sbuf", [128, C], "float32"), "sc": ("sbuf", [128, C], "float32"),
+    "SEL0": ("sbuf", [128, C], "float32"), "SEL1": ("sbuf", [128, C], "float32"), "SEL2": ("sbuf", [128, C], "float32"),
+    "VAL": ("sbuf", [128, C], "float32"), "BPS": ("sbuf", [128, C], "float32"), "APS": ("sbuf", [128, C], "float32"),
+    "VBP": ("sbuf", [128, C], "float32"),
+    "RC": ("sbuf", [128, 2 * C], "float32"), "NC": ("sbuf", [128, 2 * C], "float32"),
+    "FS": ("sbuf", [128, 2 * C + 8], "float32"), "RS": ("sbuf", [128, 2 * C + 8], "float32"),
+    "CNT": ("sbuf", [128, 2 * C], "float32"), "CNTS": ("sbuf", [128, 2 * C], "float32"),
+    "upf": ("sbuf", [128, C], "bfloat16"), "lv": ("sbuf", [128, C], "bfloat16"),
+    "inv": ("sbuf", [128, 2 * C], "bfloat16"), "LS": ("sbuf", [128, C], "bfloat16"),
+    "m1": ("sbuf", [128, W16], "float32"), "m2": ("sbuf", [128, W16], "float32"), "m3": ("sbuf", [128, W16], "float32"),
+    "slw": ("sbuf", [128, W16], "uint16"),
+    "GA": ("sbuf", [128, C], "float32"), "GB": ("sbuf", [128, C], "float32"),
+    "cab": ("sbuf", [128, 2 * W16], "float32"), "tab": ("sbuf", [128, 2 * W16], "float32"),
+    "iab": ("sbuf", [128, 2 * W16], "int32"), "jab": ("sbuf", [128, 2 * W16], "int32"),
+    "ps1": ("sbuf", [128, W16], "float32"), "pos2": ("sbuf", [128, W16], "float32"), "p2u": ("sbuf", [128, W16], "uint16"),
+    "of": ("sbuf", [128, W16], "float32"), "ow": ("sbuf", [128, W16], "uint16"),
+    "af": ("sbuf", [128, W16], "float32"), "aw": ("sbuf", [128, W16], "uint16"),
+    "bpf": ("sbuf", [128, W16], "float32"), "q1": ("sbuf", [128, W16], "float32"), "q2": ("sbuf", [128, W16], "float32"),
+    "q3": ("sbuf", [128, W16], "float32"), "dpos": ("sbuf", [128, W16], "float32"),
+    "TH": ("sbuf", [128, 4 * C], "bfloat16"), "THP": ("sbuf", [128, 4 * C], "bfloat16"),
+    "TB": ("sbuf", [128, 4 * C], "bfloat16"), "TBP": ("sbuf", [128, 4 * C], "bfloat16"),
+    "Z": ("sbuf", [128, 4 * C], "bfloat16"), "HH": ("sbuf", [128, 4 * C], "bfloat16"),
+    "ysb": ("sbuf", [128, C], "float32"), "nrs": ("sbuf", [128, C], "float32"),
+    "PA": ("psum", [128, 2048], "float32"), "PB": ("psum", [128, 1024], "float32"), "PS": ("psum", [128, 1024], "float32"),
+}
+for _k in range(1, ROUNDS + 2):
+    SCRATCH["xq%d" % _k] = ("sbuf", [128, C], F8)
+    SCRATCH["xs%d" % _k] = ("sbuf", [128, C], "uint8")
+for _k in range(1, ROUNDS + 1):
+    SCRATCH["lq%d" % _k] = ("sbuf", [128, C], F8)
+    SCRATCH["ls%d" % _k] = ("sbuf", [128, C], "uint8")
+    SCRATCH["abw%d" % _k] = ("sbuf", [128, 2 * W16], "uint16")
+    SCRATCH["lab%d" % _k] = ("sbuf", [128, 2 * W16], "uint16")
+    SCRATCH["lnx%d" % _k] = ("sbuf", [128, 2 * W16], "uint16")
+
+LOADS = ["nx", "x", "u", "ws", "wc", "v", "y0", "y1", "nr", "oc", "osc0", "osc1", "osc2", "osc3"]
+SEMAPHORES = ["cv", "cs", "ct", "cg"] + ["d_" + n for n in LOADS]
+REMOTE = ["nx"] + [n + str(k) for k in (1, 2, 3) for n in ("q", "s", "ab", "nx")]
+SEMAPHORES += ["r_" + n for n in REMOTE] + ["l_" + n for n in REMOTE]
+
+
+def rank_program(g, core, T, topo):
+    rank = T.rank_of(core)
+    if rank is None:
+        return
+    A = AluOpType
+    AF = ActivationFunctionType
+    eng = {"v": g.vector, "s": g.scalar, "t": g.tensor, "g": g, "y": g.sync}
+    total, know = {}, {q: {} for q in eng}
+    writes, reads = {}, {}
+
+    def norm(k):
+        return k if isinstance(k, tuple) else (k, 0, 1 << 20)
+
+    def conflicts(table, k):
+        return [e for e in table.get(k[0], []) if e[0] < k[2] and k[1] < e[1]]
+
+    def order(q, rd, wr):
+        need = []
+        for k in rd:
+            need += [e[2] for e in conflicts(writes, k)]
+            if k[0][0] == "P" and k[0] in ("PA", "PB", "PS"):
+                need += [e[2] for e in conflicts(reads, k) if e[2][3] != q]
+        for k in wr:
+            need += [e[2] for e in conflicts(writes, k)]
+            need += [e[2] for e in conflicts(reads, k) if e[2][3] != q]
+        kn = know[q]
+        want = {}
+        for sem, val, clock, _ in need:
+            if kn.get(sem, 0) < val and want.get(sem, (0,))[0] < val:
+                want[sem] = (val, clock)
+        for sem in list(want):
+            if any(o != sem and want[o][1].get(sem, 0) >= want[sem][0] for o in want):
+                del want[sem]
+        for sem, (val, clock) in want.items():
+            eng[q].wait_ge(T.sem[sem], val)
+            for s2, v2 in clock.items():
+                kn[s2] = max(kn.get(s2, 0), v2)
+            kn[sem] = max(kn.get(sem, 0), val)
+
+    def note(q, sem, inc, rd, wr):
+        total[sem] = total.get(sem, 0) + inc
+        clock = dict(know[q])
+        clock[sem] = total[sem]
+        ev = (sem, total[sem], clock, q)
+        for k in wr:
+            old = []
+            for e in writes.get(k[0], []):
+                if not (k[1] <= e[0] and e[1] <= k[2]):
+                    old.append(e)
+            writes[k[0]] = old + [(k[1], k[2], ev)]
+            reads[k[0]] = [e for e in reads.get(k[0], []) if not (k[1] <= e[0] and e[1] <= k[2])]
+        for k in rd:
+            reads[k[0]] = reads.get(k[0], []) + [(k[1], k[2], ev)]
+
+    COUNT = {"v": "cv", "s": "cs", "t": "ct", "g": "cg"}
+
+    def op(q, call, rd, wr):
+        rd, wr = [norm(k) for k in rd], [norm(k) for k in wr]
+        order(q, rd, wr)
+        call().then_inc(T.sem[COUNT[q]], 1)
+        note(q, COUNT[q], 1, rd, wr)
+
+    def dma(q, name, out, in_, rd, wr):
+        rd, wr = [norm(k) for k in rd], [norm(k) for k in wr]
+        order(q, rd, wr)
+        eng[q].dma_start(out, in_).then_inc(T.sem["d_" + name], 16)
+        note(q, "d_" + name, 16, rd, wr)
+
+    def send(name, dst, out, in_, rd):
+        order("g", [norm(rd)], [])
+        rid, pid = topo.addr(dst)[:2]
+        g.remote_dma(out, in_, T.sem["r_" + name], T.sem["l_" + name], pid, rid, topo.mask(core, dst))
+        note("g", "l_" + name, len(topo.engines(core, dst)), [norm(rd)], [])
+
+    def arrives(name, src, buf):
+        n = len(topo.engines(src, core))
+        total["r_" + name] = n
+        writes[buf] = [(0, 1 << 20, ("r_" + name, n, {"r_" + name: n}, "x"))]
+
+    partner = [T.cores[rank ^ m] for m in MASKS]
+    for k in (1, 2, 3):
+        arrives("q%d" % k, partner[k - 1], "lq%d" % k)
+        arrives("s%d" % k, partner[k - 1], "ls%d" % k)
+        arrives("ab%d" % k, partner[k - 1], "lab%d" % k)
+    arrives("nx", partner[0], "lnxi")
+    for k in (2, 3):
+        arrives("nx%d" % k, partner[k - 1], "lnx%d" % k)
+
+    V, S = g.vector, g.scalar
+
+    def ts(out, in0, s1, s2, o0, o1, rd, wr):
+        if o1 is None:
+            op("v", lambda: V.tensor_scalar(out, in0, s1, None, o0), rd, wr)
+        else:
+            op("v", lambda: V.tensor_scalar(out, in0, s1, s2, o0, o1), rd, wr)
+
+    def tt(out, in0, in1, o, rd, wr):
+        op("v", lambda: V.tensor_tensor(out, in0, in1, o), rd, wr)
+
+    def vcopy(out, in_, rd, wr):
+        op("v", lambda: V.tensor_copy(out, in_), rd, wr)
+
+    def scan(out, d0, d1, init, o0, o1, rd, wr):
+        op("v", lambda: V.tensor_tensor_scan(out, d0, d1, init, o0, o1), rd, wr)
+
+    def act(out, in_, rd, wr, scale=1.0, bias=0.0):
+        if bias != 0.0:
+            op("s", lambda: S.activation(out, in_, AF.Identity, bias=bias, scale=scale), rd, wr)
+        elif scale != 1.0:
+            op("s", lambda: S.activation(out, in_, AF.Copy, scale=scale), rd, wr)
+        else:
+            op("s", lambda: S.activation(out, in_, AF.Copy), rd, wr)
+
+    def quant(codes, plane, tile, lo, hi, key, at=None):
+        src = T[tile][:, 4 * lo:4 * hi] if at is None else T[tile][:, at:at + 4 * (hi - lo)]
+        op("v", lambda: V.quantize_mx(T[codes][:, lo:hi], T[plane][:, lo:hi], src),
+           [key], [(codes, lo, hi), (plane, lo, hi)])
+
+    def mm(out, pkey, l, ls, a, r, rs, lo, hi):
+        op("t", lambda: g.tensor.matmul_mx(out, T[l][:, a:a + 128], T[ls][:, a:a + 128], T[r][:, lo:hi], T[rs][:, lo:hi], True, True),
+           [(l, a, a + 128), (ls, a, a + 128), (r, lo, hi), (rs, lo, hi)], [pkey])
+
+    rot = [0]
+
+    def sel(src, key):
+        n = "SEL%d" % (rot[0] % 3)
+        rot[0] += 1
+        scan(T[n][:], T.SELD[:], src, 0.0, A.add, A.max, ["SELD", key], [n])
+        return T[n][:, 15:C:16], n
+
+    dma("y", "nx", T.nxi[:], T.nx[:], [], ["nxi"])
+    dma("s", "x", T.X0[:], T.x[:], [], ["X0"])
+    dma("y", "u", T.ut[:], T.u[:], [], ["ut"])
+    dma("y", "ws", T.wsq[:], T.ws[:], [], ["wsq"])
+    dma("y", "wc", T.wq[:].bitcast(dt.uint8), T.wc[:], [], ["wq"])
+    dma("y", "v", T.vt[:], T.v[:], [], ["vt"])
+
+    def iota(name, pattern, base, mult, exact=True):
+        if exact:
+            op("g", lambda: g.iota(T[name][:], pattern, base, mult), [], [name])
+        else:
+            op("g", lambda: g.iota(T[name][:], pattern, base, mult, allow_small_or_imprecise_dtypes=True), [], [name])
+
+    iota("pi", [[0, 1]], 0, 1)
+    iota("J16", [[0, W16], [1, 16]], 0, 0, False)
+    iota("C16", [[16, W16]], 0, 0, False)
+    iota("IOTA", [[1, C]], 0, 0, False)
+    send("nx", partner[0], T.lnxi[:], T.nxi[:], "nxi")
+    iota("EW", [[1, 516]], -4, -4, False)
+
+    ts(T.pj[:], T.pi[:], 15, None, A.bitwise_and, None, ["pi"], ["pj"])
+    vcopy(T.p16[:], T.pj[:], ["pj"], ["p16"])
+    ts(T.dd[:], T.J16[:], T.p16[:, 0:1], None, A.subtract, None, ["J16", "p16"], ["dd"])
+    ts(T.off[:], T.p16[:], 15.0, K, A.is_lt, A.mult, ["p16"], ["off"])
+    ts(T.jw[:], T.C16[:], T.p16[:, 0:1], None, A.add, None, ["C16", "p16"], ["jw"])
+    ts(T.t1[:], T.dd[:], 0.0, NEG, A.is_le, A.mult, ["dd"], ["t1"])
+    ts(T.t2[:], T.dd[:], 1.0, K, A.is_equal, A.mult, ["dd"], ["t2"])
+    ts(T.msk[:], T.jw[:], 0.0, None, A.not_equal, None, ["jw"], ["msk"])
+    tt(T.SELD[:], T.t1[:], T.t2[:], A.add, ["t1", "t2"], ["SELD"])
+    op("v", lambda: V.memset(T.Da[:], -1024.0), [], ["Da"])
+    op("v", lambda: V.memset(T.Da[:, 0:1], 0.0), [], ["Da"])
+    tt(T.L0f[:], T.nxi[:], T.msk[:], A.mult, ["nxi", "msk"], ["L0f"])
+    vcopy(T.La[:], T.L0f[:], ["L0f"], ["La"])
+
+    def consts():
+        ts(T.SELB[:], T.SELD[:], 2.0 ** -19, None, A.mult, None, ["SELD"], ["SELB"])
+        ts(T.thrB[:], T.off[:], 2.0 ** -19, 0.5, A.mult, A.add, ["off"], ["thrB"])
+        ts(T.thr2[:], T.off[:], 400000.0, None, A.add, None, ["off"], ["thr2"])
+        ts(T.thr3[:], T.off[:], 600000.0, None, A.subtract, None, ["off"], ["thr3"])
+        ts(T.offj[:], T.jw[:], T.off[:, 0:1], None, A.add, None, ["jw", "off"], ["offj"])
+        ts(T.offi[:], T.jw[:], 1024.0, T.off[:, 0:1], A.mult, A.add, ["jw", "off"], ["offi"])
+        vcopy(T.l16[:], T.C16[:], ["C16"], ["l16"])
+        op("v", lambda: V.memset(T.ONES[:], 1.0), [], ["ONES"])
+        op("v", lambda: V.memset(T.FS[:, 0:1], -float(2 ** 20)), [], [("FS", 0, 1)])
+        op("v", lambda: V.memset(T.RS[:, 2 * C + 7:2 * C + 8], float(2 ** 19)), [], [("RS", 2 * C + 7, 2 * C + 8)])
+        act(T.CODD[:], T.IOTA[:], ["IOTA"], ["CODD"], scale=1024.0, bias=512.0)
+        act(T.VC[:], T.IOTA[:], ["IOTA"], ["VC"], bias=351.0 * 1024.0)
+
+    def tiles():
+        quant("uq", "uqs", "ut", 0, 128, "ut")
+        vcopy(T.up16[:, 0:128].bitcast(dt.uint32), T.uq[:, 0:128].bitcast(dt.uint32).indirect(T.l16[:, 0:8]), ["uq", "l16"], ["up16"])
+        vcopy(T.up16s[:, 0:128], T.uqs[:, 0:128].indirect(T.l16[:, 0:8]), ["uqs", "l16"], ["up16s"])
+        ts(T.EB[:], T.EW[:], 0.0, None, A.is_equal, None, ["EW"], ["EB"])
+        for b in range(4):
+            quant("eq", "eqs", "EB", 128 * b, 128 * b + 128, "EB", at=4 - b)
+
+    def front(k, c, tile):
+        lo, hi = CH[c]
+        quant("xq%d" % k, "xs%d" % k, tile, lo, hi, (tile, 4 * lo, 4 * hi))
+        if k <= ROUNDS:
+            mm(T.PS[:, 512 * c:512 * c + hi - lo], ("PS", 512 * c, 512 * c + 512), "up16", "up16s", 0, "xq%d" % k, "xs%d" % k, lo, hi)
+
+    def ship(k):
+        p = partner[k - 1]
+        send("q%d" % k, p, T["lq%d" % k][:].bitcast(dt.uint8), T["xq%d" % k][:].bitcast(dt.uint8), "xq%d" % k)
+        send("s%d" % k, p, T["ls%d" % k][:], T["xs%d" % k][:], "xs%d" % k)
+
+    def signs():
+        for c, (lo, hi) in enumerate(CH):
+            ts(T.upf[:, lo:hi], T.PS[:, 512 * c:512 * c + hi - lo], 0.0, 2.0 ** 90, A.is_gt, A.mult,
+               [("PS", 512 * c, 512 * c + 512)], [("upf", lo, hi)])
+            act(T.sc[:, lo:hi], T.PS[:, 512 * c:512 * c + hi - lo], [("PS", 512 * c, 512 * c + 512)], [("sc", lo, hi)])
+
+    def unpack(k):
+        for b in range(4):
+            mm(T.PA[:, 512 * b:512 * b + C], ("PA", 512 * b, 512 * b + 512), "eq", "eqs", 128 * b, "xq%d" % k, "xs%d" % k, 0, C)
+
+    def keep(b):
+        act(T.TH[:, C * b:C * b + C], T.PA[:, 512 * b:512 * b + C], [("PA", 512 * b, 512 * b + 512)], [("TH", C * b, C * b + C)], scale=0.5)
+
+    def unpack_far(k, b):
+        s = b % 2
+        mm(T.PB[:, 512 * s:512 * s + C], ("PB", 512 * s, 512 * s + 512), "eq", "eqs", 128 * b, "lq%d" % k, "ls%d" % k, 0, C)
+        act(T.THP[:, C * b:C * b + C], T.PB[:, 512 * s:512 * s + C], [("PB", 512 * s, 512 * s + 512)], [("THP", C * b, C * b + C)], scale=0.5)
+
+    def places():
+        src, key = sel(T.VAL[:], "VAL")
+        tt(T.ps1[:], src, T.offj[:], A.subtract, [key, "offj"], ["ps1"])
+        ts(T.p2u[:], T.ps1[:], 2.0 ** -9, None, A.mult, None, ["ps1"], ["p2u"])
+        op("v", lambda: V.tensor_copy(T.RC[:].indirect(T.p2u[:]), T.VAL[:]), ["VAL", "p2u"], ["RC"])
+        ts(T.pos2[:], T.ps1[:], 2.0 ** -9, None, A.mult, None, ["ps1"], ["pos2"])
+
+    def columns_in_order():
+        src, key = sel(T.RC[:, 0:2 * C:2], "RC")
+        tt(T.of[:], src, T.offi[:], A.subtract, [key, "offi"], ["of"])
+        vcopy(T.ow[:], T.of[:], ["of"], ["ow"])
+
+    def far_ring(lst, key):
+        act(T.APS[:], T.IOTA[:].indirect(T[lst][:, 0:W16]), ["IOTA", key], ["APS"])
+        act(T.VBP[:], T.VAL[:].indirect(T[lst][:, W16:2 * W16]), ["VAL", key], ["VBP"])
+
+    def guests():
+        tt(T.RC[:, 1:2 * C:2], T.APS[:].indirect(T.ow[:]), T.CODD[:], A.add, ["APS", "ow", "CODD"], ["RC"])
+        src, key = sel(T.RC[:, 1:2 * C:2], "RC")
+        tt(T.af[:], src, T.offi[:], A.subtract, [key, "offi"], ["af"])
+        ts(T.aw[:], T.af[:], 512.0, None, A.subtract, None, ["af"], ["aw"])
+
+    def hosts(lst, key):
+        vcopy(T.bpf[:], T[lst][:, W16:2 * W16], [key], ["bpf"])
+        src, key2 = sel(T.VBP[:], "VBP")
+        ts(T.q1[:], src, T.off[:, 0:1], None, A.subtract, None, [key2, "off"], ["q1"])
+        tt(T.q2[:], T.q1[:], T.bpf[:], A.subtract, ["q1", "bpf"], ["q2"])
+        ts(T.q3[:], T.q2[:], 2.0 ** -9, 1.0, A.mult, A.add, ["q2"], ["q3"])
+        tt(T.dpos[:], T.q3[:], T.pos2[:], A.subtract, ["q3", "pos2"], ["dpos"])
+
+    def negatives():
+        act(T.NC[:], T.RC[:], ["RC"], ["NC"], bias=-float(2 ** 19))
+
+    def splice(k, lst, key):
+        tt(T.lv[:], T.upf[:].indirect(T[lst][:, W16:2 * W16]), T.sc[:], A.is_lt, ["upf", "sc", key], ["lv"])
+        keep(0)
+        keep(1)
+        act(T.inv[:, 0:2 * C:2], T.lv[:].indirect(T.ow[:]), ["lv", "ow"], ["inve"])
+        ts(T.inv[:, 1:2 * C:2], T.lv[:].indirect(T.aw[:]), -1.0, 1.0, A.mult, A.add, ["lv", "aw"], ["invo"])
+        scan(T.LS[:], T.SELB[:], T.lv[:], 0.0, A.add, A.max, ["SELB", "lv"], ["LS"])
+        ts(T.m1[:], T.LS[:, 15:C:16], T.thrB[:, 0:1], None, A.is_ge, None, ["LS", "thrB"], ["m1"])
+        tt(T.m2[:], T.m1[:], T.dpos[:], A.mult, ["m1", "dpos"], ["m2"])
+        tt(T.m3[:], T.m2[:], T.pos2[:], A.add, ["m2", "pos2"], ["m3"])
+        vcopy(T.slw[:], T.m3[:], ["m3"], ["slw"])
+        keep(2)
+        keep(3)
+        scan(T.FS[:, 1:2 * C + 1], T.inv[:], T.NC[:], -float(2 ** 20), A.mult, A.min, ["inve", "invo", "NC"], [("FS", 1, 2 * C + 8)])
+        act(T.GB[:], T.FS[:, 0:2 * C].indirect(T.slw[:]), ["FS", "slw"], ["GB"])
+        scan(T.RS[:, 2 * C + 6:6:-1], T.inv[:, ::-1], T.RC[:, ::-1], float(2 ** 19), A.mult, A.max,
+             ["inve", "invo", "RC"], [("RS", 0, 2 * C + 7)])
+        act(T.GA[:], T.RS[:, 8:2 * C + 8].indirect(T.slw[:]), ["RS", "slw"], ["GA"])
+        sb, kb = sel(T.GB[:], "GB")
+        ts(T.cab[:, W16:2 * W16], sb, T.off[:, 0:1], None, A.subtract, None, [kb, "off"], [("cab", W16, 2 * W16)])
+        ts(T.tab[:, W16:2 * W16], sb, T.thr3[:, 0:1], T.FS[:, 2 * C:2 * C + 1], A.is_le, A.mult, [kb, "thr3", "FS"], [("tab", W16, 2 * W16)])
+        sa, ka = sel(T.GA[:], "GA")
+        ts(T.cab[:, 0:W16], sa, T.off[:, 0:1], None, A.subtract, None, [ka, "off"], [("cab", 0, W16)])
+        ts(T.tab[:, 0:W16], sa, T.thr2[:, 0:1], T.RS[:, 7:8], A.is_ge, A.mult, [ka, "thr2", "RS"], [("tab", 0, W16)])
+        tt(T.iab[:], T.cab[:], T.tab[:], A.add, ["cab", "tab"], ["iab"])
+        ts(T.jab[:], T.iab[:], 511, None, A.bitwise_and, None, ["iab"], ["jab"])
+        abw = "abw%d" % k
+        vcopy(T[abw][:], T.jab[:], ["jab"], [abw])
+        send("ab%d" % k, partner[k - 1], T["lab%d" % k][:], T[abw][:], abw)
+        if k < ROUNDS:
+            send("nx%d" % (k + 1), partner[k], T["lnx%d" % (k + 1)][:], T[abw][:], abw)
+
+    cur, nxt = ("La", "PTa", "Da"), ("Lb", "PTb", "Db")
+    act(T.DC[:], T.Da[:], ["Da"], ["DC"])
+    act(T.PTa[:], T.IOTA[:].indirect(T.La[:]), ["IOTA", "La"], ["PTa"])
+    for i in range(9):
+        L, P, D = cur
+        L2, P2, D2 = nxt
+        if i < 8:
+            act(T[P2][:], T[P][:].indirect(T[L][:]), [P, L], [P2])
+        tt(T[D2][:], T.DC[:].indirect(T[L][:]), T[D][:], A.add, ["DC", D, L], [D2])
+        if i < 8:
+            act(T.DC[:], T[D2][:], [D2], ["DC"])
+        if i == 0:
+            consts()
+        if i == 1:
+            tiles()
+        if i == 2:
+            front(1, 0, "X0")
+            front(1, 1, "X0")
+            ship(1)
+            unpack(1)
+        if i == 3:
+            signs()
+        if i < 8:
+            src, key = sel(T[P2][:], P2)
+            ts(T[L2][:], src, T.off[:, 0:1], None, A.subtract, None, [key, "off"], [L2])
+        if i == 4:
+            vcopy(T.lnx1[:, 0:W16], T.lnxi[:], ["lnxi"], [("lnx1", 0, W16)])
+            op("v", lambda: V.tensor_copy(T.BPS[:].indirect(T.lnx1[:, 0:W16]), T.IOTA[:]), ["IOTA", ("lnx1", 0, W16)], ["BPS"])
+            src, key = sel(T.BPS[:], "BPS")
+            ts(T.lnx1[:, W16:2 * W16], src, T.off[:, 0:1], None, A.subtract, None, [key, "off"], [("lnx1", W16, 2 * W16)])
+        cur, nxt = nxt, cur
+    tt(T.VAL[:], T[cur[2]][:], T.VC[:], A.add, [cur[2], "VC"], ["VAL"])
+    far_ring("lnx1", "lnx1")
+    places()
+    columns_in_order()
+    guests()
+    negatives()
+    hosts("lnx1", "lnx1")
+
+    for k in range(1, ROUNDS + 1):
+        lst = "lnx%d" % k
+        if k > 1:
+            signs()
+        splice(k, lst, lst)
+        abw, lab = "abw%d" % k, "lab%d" % k
+        for b in range(4):
+            unpack_far(k, b)
+        if k < ROUNDS:
+            scan(T.CNT[:], T.ONES[:], T.inv[:], -1.0, A.add, A.subtract, ["ONES", "inve", "invo"], ["CNT"])
+            act(T.CNTS[:], T.CNT[:], ["CNT"], ["CNTS"], scale=1024.0)
+            tt(T.VAL[:], T.CNTS[:].indirect(T.slw[:]), T.IOTA[:], A.add, ["CNTS", "slw", "IOTA"], ["VAL"])
+            places()
+        else:
+            quant("vq", "vqs", "vt", 0, 128, "vt")
+            act(T.nrs[:], T.IOTA[:].indirect(T[abw][:, 0:W16]), ["IOTA", abw], ["nrs"])
+            dma("y", "nr", T.nr[:], T.nrs[0:128:16, :], ["nrs"], [])
+        for t in range(4):
+            act(T.TB[:, C * t:C * t + C], T.TH[:, C * t:C * t + C].indirect(T[abw][:, W16:2 * W16]),
+                [("TH", C * t, C * t + C), abw], [("TB", C * t, C * t + C)])
+        for c, (lo, hi) in enumerate(CH):
+            for t in range(4):
+                act(T.TBP[:, C * t + lo:C * t + hi], T.THP[:, C * t:C * t + C].indirect(T[lab][:, W16 + lo // 16:W16 + hi // 16]),
+                    [("THP", C * t, C * t + C), lab], [("TBP", C * t + lo, C * t + hi)])
+                tt(T.Z[:, 4 * lo + t:4 * hi:4], T.THP[:, C * t:C * t + C].indirect(T[lab][:, lo // 16:hi // 16]),
+                   T.TBP[:, C * t + lo:C * t + hi], A.add,
+                   [("THP", C * t, C * t + C), lab, ("TBP", C * t + lo, C * t + hi)], [("Z%d" % t, lo, hi)])
+            op("v", lambda: V.quantize_mx(T.zq[:, lo:hi], T.zqs[:, lo:hi], T.Z[:, 4 * lo:4 * hi]),
+               [("Z%d" % t, lo, hi) for t in range(4)], [("zq", lo, hi), ("zqs", lo, hi)])
+        if k < ROUNDS:
+            far_ring("lnx%d" % (k + 1), "lnx%d" % (k + 1))
+        for c, (lo, hi) in enumerate(CH):
+            for b in range(4):
+                if c == 0:
+                    P, s = "PA", b
+                else:
+                    P, s = ("PB", b) if b < 2 else ("PA", b - 2)
+                mm(T[P][:, 512 * s:512 * s + hi - lo], (P, 512 * s, 512 * s + 512), "wq", "wsq", 128 * b, "zq", "zqs", lo, hi)
+                act(T.HH[:, C * b + lo:C * b + hi], T[P][:, 512 * s:512 * s + hi - lo],
+                    [(P, 512 * s, 512 * s + 512)], [("HH", C * b + lo, C * b + hi)], scale=2.0 ** -6)
+        if k < ROUNDS:
+            columns_in_order()
+            guests()
+            hosts("lnx%d" % (k + 1), "lnx%d" % (k + 1))
+            negatives()
+        for c, (lo, hi) in enumerate(CH):
+            for t in range(4):
+                tt(T.X1[:, 4 * lo + t:4 * hi:4], T.HH[:, C * t:C * t + C].indirect(T[abw][:, lo // 16:hi // 16]),
+                   T.TB[:, C * t + lo:C * t + hi], A.add,
+                   [("HH", C * t, C * t + C), abw, ("TB", C * t, C * t + C)], [("X1_%d" % t, 4 * lo, 4 * hi)])
+            op("v", lambda: V.quantize_mx(T["xq%d" % (k + 1)][:, lo:hi], T["xs%d" % (k + 1)][:, lo:hi], T.X1[:, 4 * lo:4 * hi]),
+               [("X1_%d" % t, 4 * lo, 4 * hi) for t in range(4)], [("xq%d" % (k + 1), lo, hi), ("xs%d" % (k + 1), lo, hi)])
+            if k < ROUNDS:
+                mm(T.PS[:, 512 * c:512 * c + hi - lo], ("PS", 512 * c, 512 * c + 512), "up16", "up16s", 0, "xq%d" % (k + 1), "xs%d" % (k + 1), lo, hi)
+            else:
+                mm(T.PS[:, 512 * c:512 * c + hi - lo], ("PS", 512 * c, 512 * c + 512), "vq", "vqs", 0, "xq4", "xs4", lo, hi)
+                act(T.ysb[:, lo:hi], T.PS[:, 512 * c:512 * c + hi - lo], [("PS", 512 * c, 512 * c + 512)], [("ysb", lo, hi)])
+                dma("y", "y%d" % c, T.y[:, lo:hi], T.ysb[:, lo:hi], [("ysb", lo, hi)], [])
+        if k < ROUNDS:
+            ship(k + 1)
+            unpack(k + 1)
+    dma("y", "oc", T.oc[:], T.xq4[:].bitcast(dt.uint8), ["xq4"], [])
+    for i in range(4):
+        dma("y", "osc%d" % i, T.osc[4 * i:4 * i + 4, :], T.xs4[32 * i:32 * i + 4, :], ["xs4"], [])
+    for sem, val in total.items():
+        if know["g"].get(sem, 0) < val:
+            g.wait_ge(T.sem[sem], val)

@@ -6,7 +6,9 @@ CH = [(0, 192), (192, 352)]
 MASKS = [1, 2, 4]
 ROUNDS = 3
 W16 = C // 16
-NEG, K = -float(2 ** 22), float(2 ** 20)
+K = float(2 ** 20)
+GS = 128
+PS_ = 160
 F8 = "float8_e4m3fn_x4"
 
 SCRATCH = {
@@ -19,26 +21,27 @@ SCRATCH = {
     "vq": ("sbuf", [128, 128], F8), "vqs": ("sbuf", [128, 128], "uint8"),
     "eq": ("sbuf", [128, 512], F8), "eqs": ("sbuf", [128, 512], "uint8"),
     "zq": ("sbuf", [128, C], F8), "zqs": ("sbuf", [128, C], "uint8"),
-    "EW": ("sbuf", [128, 516], "float32"), "EB": ("sbuf", [128, 516], "bfloat16"),
+    "EB": ("sbuf", [128, 516], "bfloat16"),
     "IOTA": ("sbuf", [128, C], "float32"), "J16": ("sbuf", [128, C], "float32"),
     "pi": ("sbuf", [128, 1], "int32"), "pj": ("sbuf", [128, 1], "int32"), "p16": ("sbuf", [128, 1], "float32"),
     "C16": ("sbuf", [128, W16], "float32"), "l16": ("sbuf", [128, W16], "uint16"),
-    "dd": ("sbuf", [128, C], "float32"), "t1": ("sbuf", [128, C], "float32"), "t2": ("sbuf", [128, C], "float32"),
+    "t1": ("sbuf", [128, C], "float32"),
     "SELD": ("sbuf", [128, C], "bfloat16"), "SELB": ("sbuf", [128, C], "bfloat16"),
     "off": ("sbuf", [128, 1], "float32"), "thrB": ("sbuf", [128, 1], "float32"),
     "thr2": ("sbuf", [128, 1], "float32"), "thr3": ("sbuf", [128, 1], "float32"),
-    "jw": ("sbuf", [128, W16], "float32"), "msk": ("sbuf", [128, W16], "float32"),
-    "offj": ("sbuf", [128, W16], "float32"), "offi": ("sbuf", [128, W16], "float32"),
-    "CODD": ("sbuf", [128, C], "float32"), "VC": ("sbuf", [128, C], "float32"), "ONES": ("sbuf", [128, 2 * C], "bfloat16"),
-    "L0f": ("sbuf", [128, W16], "float32"), "La": ("sbuf", [128, W16], "uint16"), "Lb": ("sbuf", [128, W16], "uint16"),
-    "PTa": ("sbuf", [128, C], "float32"), "PTb": ("sbuf", [128, C], "float32"),
-    "Da": ("sbuf", [128, C], "float32"), "Db": ("sbuf", [128, C], "float32"), "DC": ("sbuf", [128, C], "float32"), "sc": ("sbuf", [128, C], "float32"),
+    "jw": ("sbuf", [128, W16], "float32"),
+    "offg": ("sbuf", [128, W16], "float32"), "noff": ("sbuf", [128, 1], "float32"), "p16h": ("sbuf", [128, 1], "float32"), "offi": ("sbuf", [128, W16], "float32"),
+    "CODD": ("sbuf", [128, C], "float32"), "CEV": ("sbuf", [128, C], "float32"), "ONES": ("sbuf", [128, 2 * C], "bfloat16"),
+    "La": ("sbuf", [128, W16], "uint16"), "Lb": ("sbuf", [128, W16], "uint16"),
+    "PTa": ("sbuf", [128, C], "float32"), "PTb": ("sbuf", [128, C], "float32"), "PTc": ("sbuf", [128, C], "float32"),
+    "OB": ("sbuf", [128, C], "float32"), "SELO": ("sbuf", [128, 128], "float32"), "sc": ("sbuf", [128, C], "bfloat16"),
+    "POS": ("sbuf", [128, C], "float32"), "SELP": ("sbuf", [128, C], "float32"), "posw": ("sbuf", [128, W16], "float32"),
     "SEL0": ("sbuf", [128, C], "float32"), "SEL1": ("sbuf", [128, C], "float32"), "SEL2": ("sbuf", [128, C], "float32"),
     "VAL": ("sbuf", [128, C], "float32"), "BPS": ("sbuf", [128, C], "float32"), "APS": ("sbuf", [128, C], "float32"),
     "VBP": ("sbuf", [128, C], "float32"),
     "RC": ("sbuf", [128, 2 * C], "float32"), "NC": ("sbuf", [128, 2 * C], "float32"),
     "FS": ("sbuf", [128, 2 * C + 8], "float32"), "RS": ("sbuf", [128, 2 * C + 8], "float32"),
-    "CNT": ("sbuf", [128, 2 * C], "float32"), "CNTS": ("sbuf", [128, 2 * C], "float32"),
+    "CNT": ("sbuf", [128, 2 * C], "float32"),
     "upf": ("sbuf", [128, C], "bfloat16"), "lv": ("sbuf", [128, C], "bfloat16"),
     "inv": ("sbuf", [128, 2 * C], "bfloat16"), "LS": ("sbuf", [128, C], "bfloat16"),
     "m1": ("sbuf", [128, W16], "float32"), "m2": ("sbuf", [128, W16], "float32"), "m3": ("sbuf", [128, W16], "float32"),
@@ -46,11 +49,10 @@ SCRATCH = {
     "GA": ("sbuf", [128, C], "float32"), "GB": ("sbuf", [128, C], "float32"),
     "cab": ("sbuf", [128, 2 * W16], "float32"), "tab": ("sbuf", [128, 2 * W16], "float32"),
     "iab": ("sbuf", [128, 2 * W16], "int32"), "jab": ("sbuf", [128, 2 * W16], "int32"),
-    "ps1": ("sbuf", [128, W16], "float32"), "pos2": ("sbuf", [128, W16], "float32"), "p2u": ("sbuf", [128, W16], "uint16"),
+    "p2u": ("sbuf", [128, W16], "uint16"),
     "of": ("sbuf", [128, W16], "float32"), "ow": ("sbuf", [128, W16], "uint16"),
     "af": ("sbuf", [128, W16], "float32"), "aw": ("sbuf", [128, W16], "uint16"),
-    "bpf": ("sbuf", [128, W16], "float32"), "q1": ("sbuf", [128, W16], "float32"), "q2": ("sbuf", [128, W16], "float32"),
-    "q3": ("sbuf", [128, W16], "float32"), "dpos": ("sbuf", [128, W16], "float32"),
+    "dpos": ("sbuf", [128, W16], "float32"),
     "TH": ("sbuf", [128, 4 * C], "bfloat16"), "THP": ("sbuf", [128, 4 * C], "bfloat16"),
     "TB": ("sbuf", [128, 4 * C], "bfloat16"), "TBP": ("sbuf", [128, 4 * C], "bfloat16"),
     "Z": ("sbuf", [128, 4 * C], "bfloat16"), "HH": ("sbuf", [128, 4 * C], "bfloat16"),
@@ -97,7 +99,7 @@ def rank_program(g, core, T, topo):
                 need += [e[2] for e in conflicts(reads, k) if e[2][3] != q]
         for k in wr:
             need += [e[2] for e in conflicts(writes, k)]
-            need += [e[2] for e in conflicts(reads, k) if e[2][3] != q]
+            need += [e[2] for e in conflicts(reads, k)]
         kn = know[q]
         want = {}
         for sem, val, clock, _ in need:
@@ -218,44 +220,43 @@ def rank_program(g, core, T, topo):
 
     iota("pi", [[0, 1]], 0, 1)
     iota("J16", [[0, W16], [1, 16]], 0, 0, False)
-    iota("C16", [[16, W16]], 0, 0, False)
     iota("IOTA", [[1, C]], 0, 0, False)
+    iota("C16", [[16, W16]], 0, 0, False)
     send("nx", partner[0], T.lnxi[:], T.nxi[:], "nxi")
-    iota("EW", [[1, 516]], -4, -4, False)
 
     ts(T.pj[:], T.pi[:], 15, None, A.bitwise_and, None, ["pi"], ["pj"])
-    vcopy(T.p16[:], T.pj[:], ["pj"], ["p16"])
-    ts(T.dd[:], T.J16[:], T.p16[:, 0:1], None, A.subtract, None, ["J16", "p16"], ["dd"])
-    ts(T.off[:], T.p16[:], 15.0, K, A.is_lt, A.mult, ["p16"], ["off"])
-    ts(T.jw[:], T.C16[:], T.p16[:, 0:1], None, A.add, None, ["C16", "p16"], ["jw"])
-    ts(T.t1[:], T.dd[:], 0.0, NEG, A.is_le, A.mult, ["dd"], ["t1"])
-    ts(T.t2[:], T.dd[:], 1.0, K, A.is_equal, A.mult, ["dd"], ["t2"])
-    ts(T.msk[:], T.jw[:], 0.0, None, A.not_equal, None, ["jw"], ["msk"])
-    tt(T.SELD[:], T.t1[:], T.t2[:], A.add, ["t1", "t2"], ["SELD"])
-    op("v", lambda: V.memset(T.Da[:], -1024.0), [], ["Da"])
-    op("v", lambda: V.memset(T.Da[:, 0:1], 0.0), [], ["Da"])
-    tt(T.L0f[:], T.nxi[:], T.msk[:], A.mult, ["nxi", "msk"], ["L0f"])
-    vcopy(T.La[:], T.L0f[:], ["L0f"], ["La"])
+    op("v", lambda: V.memset(T.ONES[:], 1.0), [], ["ONES"])
+    ts(T.p16h[:], T.pj[:], 0.5, None, A.add, None, ["pj"], ["p16h"])
+    ts(T.p16[:], T.pj[:], 0.0, None, A.add, None, ["pj"], ["p16"])
+    ts(T.t1[:], T.J16[:], T.p16h[:, 0:1], 2.0 ** 26, A.subtract, A.mult, ["J16", "p16h"], ["t1"])
+    ts(T.off[:], T.p16[:], -K, 15.0 * K, A.mult, A.add, ["p16"], ["off"])
+    ts(T.SELD[:], T.t1[:], K, None, A.min, None, ["t1"], ["SELD"])
+    vcopy(T.La[:], T.nxi[:], ["nxi"], ["La"])
+    op("v", lambda: V.memset(T.ow[:], 0), [], ["ow"])
+    op("v", lambda: V.memset(T.OB[:, 0:1], 0.0), [], ["OB"])
+    op("g", lambda: g.affine_select(T.EB[:], T.ONES[:, 0:516], [[1, 516]], A.is_equal, 0.0, -4, -4), ["ONES"], ["EB"])
 
     def consts():
-        ts(T.SELB[:], T.SELD[:], 2.0 ** -19, None, A.mult, None, ["SELD"], ["SELB"])
+        ts(T.noff[:], T.off[:], -1.0, None, A.mult, None, ["off"], ["noff"])
+        ts(T.jw[:], T.C16[:], T.p16[:, 0:1], None, A.add, None, ["C16", "p16"], ["jw"])
         ts(T.thrB[:], T.off[:], 2.0 ** -19, 0.5, A.mult, A.add, ["off"], ["thrB"])
         ts(T.thr2[:], T.off[:], 400000.0, None, A.add, None, ["off"], ["thr2"])
         ts(T.thr3[:], T.off[:], 600000.0, None, A.subtract, None, ["off"], ["thr3"])
-        ts(T.offj[:], T.jw[:], T.off[:, 0:1], None, A.add, None, ["jw", "off"], ["offj"])
         ts(T.offi[:], T.jw[:], 1024.0, T.off[:, 0:1], A.mult, A.add, ["jw", "off"], ["offi"])
         vcopy(T.l16[:], T.C16[:], ["C16"], ["l16"])
-        op("v", lambda: V.memset(T.ONES[:], 1.0), [], ["ONES"])
+        ts(T.offg[:], T.offi[:], 512.0, None, A.add, None, ["offi"], ["offg"])
         op("v", lambda: V.memset(T.FS[:, 0:1], -float(2 ** 20)), [], [("FS", 0, 1)])
         op("v", lambda: V.memset(T.RS[:, 2 * C + 7:2 * C + 8], float(2 ** 19)), [], [("RS", 2 * C + 7, 2 * C + 8)])
+
+    def tables():
+        act(T.SELB[:], T.SELD[:], ["SELD"], ["SELB"], scale=2.0 ** -19)
         act(T.CODD[:], T.IOTA[:], ["IOTA"], ["CODD"], scale=1024.0, bias=512.0)
-        act(T.VC[:], T.IOTA[:], ["IOTA"], ["VC"], bias=351.0 * 1024.0)
+        act(T.CEV[:], T.IOTA[:], ["IOTA"], ["CEV"], scale=1024.0)
 
     def tiles():
         quant("uq", "uqs", "ut", 0, 128, "ut")
         vcopy(T.up16[:, 0:128].bitcast(dt.uint32), T.uq[:, 0:128].bitcast(dt.uint32).indirect(T.l16[:, 0:8]), ["uq", "l16"], ["up16"])
-        vcopy(T.up16s[:, 0:128], T.uqs[:, 0:128].indirect(T.l16[:, 0:8]), ["uqs", "l16"], ["up16s"])
-        ts(T.EB[:], T.EW[:], 0.0, None, A.is_equal, None, ["EW"], ["EB"])
+        act(T.up16s[:, 0:128], T.uqs[:, 0:128].indirect(T.l16[:, 0:8]), ["uqs", "l16"], ["up16s"])
         for b in range(4):
             quant("eq", "eqs", "EB", 128 * b, 128 * b + 128, "EB", at=4 - b)
 
@@ -272,9 +273,9 @@ def rank_program(g, core, T, topo):
 
     def signs():
         for c, (lo, hi) in enumerate(CH):
-            ts(T.upf[:, lo:hi], T.PS[:, 512 * c:512 * c + hi - lo], 0.0, 2.0 ** 90, A.is_gt, A.mult,
-               [("PS", 512 * c, 512 * c + 512)], [("upf", lo, hi)])
-            act(T.sc[:, lo:hi], T.PS[:, 512 * c:512 * c + hi - lo], [("PS", 512 * c, 512 * c + 512)], [("sc", lo, hi)])
+            op("s", lambda: S.activation(T.sc[:, lo:hi], T.PS[:, 512 * c:512 * c + hi - lo], AF.Sign),
+               [("PS", 512 * c, 512 * c + 512)], [("sc", lo, hi)])
+            ts(T.upf[:, lo:hi], T.sc[:, lo:hi], 0.0, None, A.max, None, [("sc", lo, hi)], [("upf", lo, hi)])
 
     def unpack(k):
         for b in range(4):
@@ -289,11 +290,13 @@ def rank_program(g, core, T, topo):
         act(T.THP[:, C * b:C * b + C], T.PB[:, 512 * s:512 * s + C], [("PB", 512 * s, 512 * s + 512)], [("THP", C * b, C * b + C)], scale=0.5)
 
     def places():
-        src, key = sel(T.VAL[:], "VAL")
-        tt(T.ps1[:], src, T.offj[:], A.subtract, [key, "offj"], ["ps1"])
-        ts(T.p2u[:], T.ps1[:], 2.0 ** -9, None, A.mult, None, ["ps1"], ["p2u"])
+        scan(T.SELP[:], T.SELD[:], T.POS[:], 0.0, A.add, A.max, ["SELD", "POS"], ["SELP"])
+        op("s", lambda: S.activation(T.posw[:], T.SELP[:, 15:C:16], AF.Identity, bias=T.noff[:, 0:1]), ["SELP", "noff"], ["posw"])
+
+    def lay_order():
+        tt(T.VAL[:], T.POS[:], T.IOTA[:], A.add, ["POS", "IOTA"], ["VAL"])
+        ts(T.p2u[:], T.SELP[:, 15:C:16], T.off[:, 0:1], 2.0 ** -9, A.subtract, A.mult, ["SELP", "off"], ["p2u"])
         op("v", lambda: V.tensor_copy(T.RC[:].indirect(T.p2u[:]), T.VAL[:]), ["VAL", "p2u"], ["RC"])
-        ts(T.pos2[:], T.ps1[:], 2.0 ** -9, None, A.mult, None, ["ps1"], ["pos2"])
 
     def columns_in_order():
         src, key = sel(T.RC[:, 0:2 * C:2], "RC")
@@ -302,21 +305,19 @@ def rank_program(g, core, T, topo):
 
     def far_ring(lst, key):
         act(T.APS[:], T.IOTA[:].indirect(T[lst][:, 0:W16]), ["IOTA", key], ["APS"])
-        act(T.VBP[:], T.VAL[:].indirect(T[lst][:, W16:2 * W16]), ["VAL", key], ["VBP"])
+
+    def far_places(lst, key):
+        act(T.VBP[:], T.POS[:].indirect(T[lst][:, W16:2 * W16]), ["POS", key], ["VBP"], bias=512.0)
 
     def guests():
         tt(T.RC[:, 1:2 * C:2], T.APS[:].indirect(T.ow[:]), T.CODD[:], A.add, ["APS", "ow", "CODD"], ["RC"])
         src, key = sel(T.RC[:, 1:2 * C:2], "RC")
-        tt(T.af[:], src, T.offi[:], A.subtract, [key, "offi"], ["af"])
-        ts(T.aw[:], T.af[:], 512.0, None, A.subtract, None, ["af"], ["aw"])
+        tt(T.af[:], src, T.offg[:], A.subtract, [key, "offg"], ["af"])
+        vcopy(T.aw[:], T.af[:], ["af"], ["aw"])
 
-    def hosts(lst, key):
-        vcopy(T.bpf[:], T[lst][:, W16:2 * W16], [key], ["bpf"])
-        src, key2 = sel(T.VBP[:], "VBP")
-        ts(T.q1[:], src, T.off[:, 0:1], None, A.subtract, None, [key2, "off"], ["q1"])
-        tt(T.q2[:], T.q1[:], T.bpf[:], A.subtract, ["q1", "bpf"], ["q2"])
-        ts(T.q3[:], T.q2[:], 2.0 ** -9, 1.0, A.mult, A.add, ["q2"], ["q3"])
-        tt(T.dpos[:], T.q3[:], T.pos2[:], A.subtract, ["q3", "pos2"], ["dpos"])
+    def hosts():
+        src, key = sel(T.VBP[:], "VBP")
+        tt(T.dpos[:], src, T.SELP[:, 15:C:16], A.subtract, [key, "SELP"], ["dpos"])
 
     def negatives():
         act(T.NC[:], T.RC[:], ["RC"], ["NC"], bias=-float(2 ** 19))
@@ -326,24 +327,25 @@ def rank_program(g, core, T, topo):
         keep(0)
         keep(1)
         act(T.inv[:, 0:2 * C:2], T.lv[:].indirect(T.ow[:]), ["lv", "ow"], ["inve"])
-        ts(T.inv[:, 1:2 * C:2], T.lv[:].indirect(T.aw[:]), -1.0, 1.0, A.mult, A.add, ["lv", "aw"], ["invo"])
+        act(T.inv[:, 1 + 2 * GS:2 * C:2], T.lv[:].indirect(T.aw[:, GS // 16:W16]), ["lv", "aw"], ["invp"], scale=-1.0, bias=1.0)
+        ts(T.inv[:, 1:2 * GS:2], T.lv[:].indirect(T.aw[:, 0:GS // 16]), -1.0, 1.0, A.mult, A.add, ["lv", "aw"], ["invo"])
         scan(T.LS[:], T.SELB[:], T.lv[:], 0.0, A.add, A.max, ["SELB", "lv"], ["LS"])
         ts(T.m1[:], T.LS[:, 15:C:16], T.thrB[:, 0:1], None, A.is_ge, None, ["LS", "thrB"], ["m1"])
         tt(T.m2[:], T.m1[:], T.dpos[:], A.mult, ["m1", "dpos"], ["m2"])
-        tt(T.m3[:], T.m2[:], T.pos2[:], A.add, ["m2", "pos2"], ["m3"])
-        vcopy(T.slw[:], T.m3[:], ["m3"], ["slw"])
+        tt(T.m3[:], T.m2[:], T.posw[:], A.add, ["m2", "posw"], ["m3"])
+        ts(T.slw[:], T.m3[:], 2.0 ** -9, None, A.mult, None, ["m3"], ["slw"])
         keep(2)
         keep(3)
-        scan(T.FS[:, 1:2 * C + 1], T.inv[:], T.NC[:], -float(2 ** 20), A.mult, A.min, ["inve", "invo", "NC"], [("FS", 1, 2 * C + 8)])
+        scan(T.FS[:, 1:2 * C + 1], T.inv[:], T.NC[:], -float(2 ** 20), A.mult, A.min, ["inve", "invo", "invp", "NC"], [("FS", 1, 2 * C + 8)])
         act(T.GB[:], T.FS[:, 0:2 * C].indirect(T.slw[:]), ["FS", "slw"], ["GB"])
         scan(T.RS[:, 2 * C + 6:6:-1], T.inv[:, ::-1], T.RC[:, ::-1], float(2 ** 19), A.mult, A.max,
-             ["inve", "invo", "RC"], [("RS", 0, 2 * C + 7)])
+             ["inve", "invo", "invp", "RC"], [("RS", 0, 2 * C + 7)])
         act(T.GA[:], T.RS[:, 8:2 * C + 8].indirect(T.slw[:]), ["RS", "slw"], ["GA"])
         sb, kb = sel(T.GB[:], "GB")
-        ts(T.cab[:, W16:2 * W16], sb, T.off[:, 0:1], None, A.subtract, None, [kb, "off"], [("cab", W16, 2 * W16)])
+        op("s", lambda: S.activation(T.cab[:, W16:2 * W16], sb, AF.Identity, bias=T.noff[:, 0:1]), [kb, "noff"], [("cab", W16, 2 * W16)])
         ts(T.tab[:, W16:2 * W16], sb, T.thr3[:, 0:1], T.FS[:, 2 * C:2 * C + 1], A.is_le, A.mult, [kb, "thr3", "FS"], [("tab", W16, 2 * W16)])
         sa, ka = sel(T.GA[:], "GA")
-        ts(T.cab[:, 0:W16], sa, T.off[:, 0:1], None, A.subtract, None, [ka, "off"], [("cab", 0, W16)])
+        op("s", lambda: S.activation(T.cab[:, 0:W16], sa, AF.Identity, bias=T.noff[:, 0:1]), [ka, "noff"], [("cab", 0, W16)])
         ts(T.tab[:, 0:W16], sa, T.thr2[:, 0:1], T.RS[:, 7:8], A.is_ge, A.mult, [ka, "thr2", "RS"], [("tab", 0, W16)])
         tt(T.iab[:], T.cab[:], T.tab[:], A.add, ["cab", "tab"], ["iab"])
         ts(T.jab[:], T.iab[:], 511, None, A.bitwise_and, None, ["iab"], ["jab"])
@@ -353,19 +355,28 @@ def rank_program(g, core, T, topo):
         if k < ROUNDS:
             send("nx%d" % (k + 1), partner[k], T["lnx%d" % (k + 1)][:], T[abw][:], abw)
 
-    cur, nxt = ("La", "PTa", "Da"), ("Lb", "PTb", "Db")
-    act(T.DC[:], T.Da[:], ["Da"], ["DC"])
-    act(T.PTa[:], T.IOTA[:].indirect(T.La[:]), ["IOTA", "La"], ["PTa"])
+    def jump(out, win, lst):
+        act(T[out][:, PS_:C], T[win][:].indirect(T[lst][:, PS_ // 16:W16]), [win, lst], [(out, PS_, C)])
+        vcopy(T[out][:, 0:PS_], T[win][:].indirect(T[lst][:, 0:PS_ // 16]), [win, lst], [(out, 0, PS_)])
+
+    jump("PTa", "IOTA", "La")
     for i in range(9):
-        L, P, D = cur
-        L2, P2, D2 = nxt
+        L, L2 = ("La", "Lb") if i % 2 == 0 else ("Lb", "La")
+        P, P2 = (("PTa", "PTb"), ("PTb", "PTc"), ("PTc", "PTa"))[i % 3]
+        m = 2 ** i
+        n = min(max(16, m), C - m)
         if i < 8:
-            act(T[P2][:], T[P][:].indirect(T[L][:]), [P, L], [P2])
-        tt(T[D2][:], T.DC[:].indirect(T[L][:]), T[D][:], A.add, ["DC", D, L], [D2])
-        if i < 8:
-            act(T.DC[:], T[D2][:], [D2], ["DC"])
+            jump(P2, P, L)
+        act(T.OB[:, m:m + n], T[P][:].indirect(T.ow[:, 0:n // 16]), [P, "ow"], ["OB"])
+        if i < 7:
+            src, key = sel(T[P2][:], P2)
+            ts(T[L2][:], src, T.off[:, 0:1], None, A.subtract, None, [key, "off"], [L2])
+        a = 0 if m < 16 else m
+        scan(T.SELO[:, 0:n], T.SELD[:, 0:n], T.OB[:, a:a + n], 0.0, A.add, A.max, ["SELD", "OB"], ["SELO"])
+        ts(T.ow[:, a // 16:(a + n) // 16], T.SELO[:, 15:n:16], T.off[:, 0:1], None, A.subtract, None, ["SELO", "off"], ["ow"])
         if i == 0:
             consts()
+            tables()
         if i == 1:
             tiles()
         if i == 2:
@@ -375,22 +386,20 @@ def rank_program(g, core, T, topo):
             unpack(1)
         if i == 3:
             signs()
-        if i < 8:
-            src, key = sel(T[P2][:], P2)
-            ts(T[L2][:], src, T.off[:, 0:1], None, A.subtract, None, [key, "off"], [L2])
         if i == 4:
             vcopy(T.lnx1[:, 0:W16], T.lnxi[:], ["lnxi"], [("lnx1", 0, W16)])
             op("v", lambda: V.tensor_copy(T.BPS[:].indirect(T.lnx1[:, 0:W16]), T.IOTA[:]), ["IOTA", ("lnx1", 0, W16)], ["BPS"])
             src, key = sel(T.BPS[:], "BPS")
             ts(T.lnx1[:, W16:2 * W16], src, T.off[:, 0:1], None, A.subtract, None, [key, "off"], [("lnx1", W16, 2 * W16)])
-        cur, nxt = nxt, cur
-    tt(T.VAL[:], T[cur[2]][:], T.VC[:], A.add, [cur[2], "VC"], ["VAL"])
-    far_ring("lnx1", "lnx1")
-    places()
-    columns_in_order()
+        if i == 7:
+            far_ring("lnx1", "lnx1")
+    op("v", lambda: V.tensor_copy(T.POS[:].indirect(T.ow[:]), T.CEV[:]), ["ow", "CEV"], ["POS"])
+    far_places("lnx1", "lnx1")
     guests()
+    places()
+    tt(T.RC[:, 0:2 * C:2], T.OB[:], T.CEV[:], A.add, ["OB", "CEV"], ["RC"])
     negatives()
-    hosts("lnx1", "lnx1")
+    hosts()
 
     for k in range(1, ROUNDS + 1):
         lst = "lnx%d" % k
@@ -398,20 +407,28 @@ def rank_program(g, core, T, topo):
             signs()
         splice(k, lst, lst)
         abw, lab = "abw%d" % k, "lab%d" % k
-        for b in range(4):
-            unpack_far(k, b)
+
+        def own(t, q):
+            (act if q == "s" else vcopy)(T.TB[:, C * t:C * t + C], T.TH[:, C * t:C * t + C].indirect(T[abw][:, W16:2 * W16]),
+                                         [("TH", C * t, C * t + C), abw], [("TB", C * t, C * t + C)])
         if k < ROUNDS:
-            scan(T.CNT[:], T.ONES[:], T.inv[:], -1.0, A.add, A.subtract, ["ONES", "inve", "invo"], ["CNT"])
-            act(T.CNTS[:], T.CNT[:], ["CNT"], ["CNTS"], scale=1024.0)
-            tt(T.VAL[:], T.CNTS[:].indirect(T.slw[:]), T.IOTA[:], A.add, ["CNTS", "slw", "IOTA"], ["VAL"])
+            scan(T.CNT[:], T.ONES[:], T.inv[:], -1.0, A.add, A.subtract, ["ONES", "inve", "invo", "invp"], ["CNT"])
+            unpack_far(k, 0)
+            act(T.POS[:], T.CNT[:].indirect(T.slw[:]), ["CNT", "slw"], ["POS"], scale=1024.0)
+            own(0, "v")
+            for b in (1, 2, 3):
+                unpack_far(k, b)
             places()
+            lay_order()
+            own(1, "v")
+            for t in (2, 3):
+                own(t, "s")
         else:
+            for b in range(4):
+                unpack_far(k, b)
             quant("vq", "vqs", "vt", 0, 128, "vt")
-            act(T.nrs[:], T.IOTA[:].indirect(T[abw][:, 0:W16]), ["IOTA", abw], ["nrs"])
-            dma("y", "nr", T.nr[:], T.nrs[0:128:16, :], ["nrs"], [])
-        for t in range(4):
-            act(T.TB[:, C * t:C * t + C], T.TH[:, C * t:C * t + C].indirect(T[abw][:, W16:2 * W16]),
-                [("TH", C * t, C * t + C), abw], [("TB", C * t, C * t + C)])
+            for t in range(4):
+                own(t, "v")
         for c, (lo, hi) in enumerate(CH):
             for t in range(4):
                 act(T.TBP[:, C * t + lo:C * t + hi], T.THP[:, C * t:C * t + C].indirect(T[lab][:, W16 + lo // 16:W16 + hi // 16]),
@@ -423,6 +440,10 @@ def rank_program(g, core, T, topo):
                [("Z%d" % t, lo, hi) for t in range(4)], [("zq", lo, hi), ("zqs", lo, hi)])
         if k < ROUNDS:
             far_ring("lnx%d" % (k + 1), "lnx%d" % (k + 1))
+            far_places("lnx%d" % (k + 1), "lnx%d" % (k + 1))
+        else:
+            act(T.nrs[:], T.IOTA[:].indirect(T[abw][:, 0:W16]), ["IOTA", abw], ["nrs"])
+            dma("y", "nr", T.nr[:], T.nrs[0:128:16, :], ["nrs"], [])
         for c, (lo, hi) in enumerate(CH):
             for b in range(4):
                 if c == 0:
@@ -435,7 +456,7 @@ def rank_program(g, core, T, topo):
         if k < ROUNDS:
             columns_in_order()
             guests()
-            hosts("lnx%d" % (k + 1), "lnx%d" % (k + 1))
+            hosts()
             negatives()
         for c, (lo, hi) in enumerate(CH):
             for t in range(4):

@@ -1,19 +1,18 @@
-from concourse.bass import DstId, RemoteDMATransfer
 from concourse.mybir import dt, AluOpType, ActivationFunctionType
 
 C = 352
-CH = [(0, 192), (192, 352)]
+CH = [(0, 224), (224, 352)]
+CH0 = [(0, 192), (192, 352)]
 MASKS = [1, 2, 4]
 ROUNDS = 3
 W16 = C // 16
 K = float(2 ** 20)
-GS = 128
-PS_ = 160
+GS = 192
+TOP = 6
 F8 = "float8_e4m3fn_x4"
 
 SCRATCH = {
     "nxi": ("sbuf", [128, W16], "int32"), "lnxi": ("sbuf", [128, W16], "int32"),
-    "X0": ("sbuf", [128, 4 * C], "bfloat16"), "X1": ("sbuf", [128, 4 * C], "bfloat16"),
     "ut": ("sbuf", [128, 512], "bfloat16"), "vt": ("sbuf", [128, 512], "bfloat16"),
     "wq": ("sbuf", [128, 512], F8), "wsq": ("sbuf", [128, 512], "uint8"),
     "uq": ("sbuf", [128, 128], F8), "uqs": ("sbuf", [128, 128], "uint8"),
@@ -21,58 +20,41 @@ SCRATCH = {
     "vq": ("sbuf", [128, 128], F8), "vqs": ("sbuf", [128, 128], "uint8"),
     "eq": ("sbuf", [128, 512], F8), "eqs": ("sbuf", [128, 512], "uint8"),
     "zq": ("sbuf", [128, C], F8), "zqs": ("sbuf", [128, C], "uint8"),
-    "EB": ("sbuf", [128, 516], "bfloat16"),
-    "IOTA": ("sbuf", [128, C], "float32"), "J16": ("sbuf", [128, C], "float32"),
-    "pi": ("sbuf", [128, 1], "int32"), "pj": ("sbuf", [128, 1], "int32"), "p16": ("sbuf", [128, 1], "float32"),
-    "C16": ("sbuf", [128, W16], "float32"), "l16": ("sbuf", [128, W16], "uint16"),
-    "t1": ("sbuf", [128, C], "float32"),
-    "SELD": ("sbuf", [128, C], "bfloat16"), "SELB": ("sbuf", [128, C], "bfloat16"),
-    "off": ("sbuf", [128, 1], "float32"), "thrB": ("sbuf", [128, 1], "float32"),
-    "thr2": ("sbuf", [128, 1], "float32"), "thr3": ("sbuf", [128, 1], "float32"),
-    "jw": ("sbuf", [128, W16], "float32"),
-    "offg": ("sbuf", [128, W16], "float32"), "noff": ("sbuf", [128, 1], "float32"), "p16h": ("sbuf", [128, 1], "float32"), "offi": ("sbuf", [128, W16], "float32"),
-    "CODD": ("sbuf", [128, C], "float32"), "CEV": ("sbuf", [128, C], "float32"), "ONES": ("sbuf", [128, 2 * C], "bfloat16"),
-    "La": ("sbuf", [128, W16], "uint16"), "Lb": ("sbuf", [128, W16], "uint16"),
-    "PTa": ("sbuf", [128, C], "float32"), "PTb": ("sbuf", [128, C], "float32"), "PTc": ("sbuf", [128, C], "float32"),
-    "OB": ("sbuf", [128, C], "float32"), "SELO": ("sbuf", [128, 128], "float32"), "sc": ("sbuf", [128, C], "bfloat16"),
-    "POS": ("sbuf", [128, C], "float32"), "SELP": ("sbuf", [128, C], "float32"), "posw": ("sbuf", [128, W16], "float32"),
-    "SEL0": ("sbuf", [128, C], "float32"), "SEL1": ("sbuf", [128, C], "float32"), "SEL2": ("sbuf", [128, C], "float32"),
-    "VAL": ("sbuf", [128, C], "float32"), "BPS": ("sbuf", [128, C], "float32"), "APS": ("sbuf", [128, C], "float32"),
-    "VBP": ("sbuf", [128, C], "float32"),
-    "RC": ("sbuf", [128, 2 * C], "float32"), "NC": ("sbuf", [128, 2 * C], "float32"),
+    "EB": ("sbuf", [128, 516], "bfloat16"), "ONES": ("sbuf", [128, 2 * C], "bfloat16"),
+    "pi": ("sbuf", [128, 1], "int32"), "pj": ("sbuf", [128, 1], "int32"),
     "FS": ("sbuf", [128, 2 * C + 8], "float32"), "RS": ("sbuf", [128, 2 * C + 8], "float32"),
-    "CNT": ("sbuf", [128, 2 * C], "float32"),
-    "upf": ("sbuf", [128, C], "bfloat16"), "lv": ("sbuf", [128, C], "bfloat16"),
-    "inv": ("sbuf", [128, 2 * C], "bfloat16"), "LS": ("sbuf", [128, C], "bfloat16"),
-    "m1": ("sbuf", [128, W16], "float32"), "m2": ("sbuf", [128, W16], "float32"), "m3": ("sbuf", [128, W16], "float32"),
-    "slw": ("sbuf", [128, W16], "uint16"),
-    "GA": ("sbuf", [128, C], "float32"), "GB": ("sbuf", [128, C], "float32"),
+    "inv": ("sbuf", [128, 2 * C], "bfloat16"),
     "cab": ("sbuf", [128, 2 * W16], "float32"), "tab": ("sbuf", [128, 2 * W16], "float32"),
     "iab": ("sbuf", [128, 2 * W16], "int32"), "jab": ("sbuf", [128, 2 * W16], "int32"),
-    "p2u": ("sbuf", [128, W16], "uint16"),
-    "of": ("sbuf", [128, W16], "float32"), "ow": ("sbuf", [128, W16], "uint16"),
-    "af": ("sbuf", [128, W16], "float32"), "aw": ("sbuf", [128, W16], "uint16"),
-    "dpos": ("sbuf", [128, W16], "float32"),
-    "TH": ("sbuf", [128, 4 * C], "bfloat16"), "THP": ("sbuf", [128, 4 * C], "bfloat16"),
-    "TB": ("sbuf", [128, 4 * C], "bfloat16"), "TBP": ("sbuf", [128, 4 * C], "bfloat16"),
-    "Z": ("sbuf", [128, 4 * C], "bfloat16"), "HH": ("sbuf", [128, 4 * C], "bfloat16"),
-    "ysb": ("sbuf", [128, C], "float32"), "nrs": ("sbuf", [128, C], "float32"),
     "PA": ("psum", [128, 2048], "float32"), "PB": ("psum", [128, 1024], "float32"), "PS": ("psum", [128, 1024], "float32"),
 }
+for _n in ("X0", "X1", "TH", "THP", "TB", "TBP", "Z", "HH"):
+    SCRATCH[_n] = ("sbuf", [128, 4 * C], "bfloat16")
+for _n in ("RC", "NC", "CNT"):
+    SCRATCH[_n] = ("sbuf", [128, 2 * C], "float32")
+for _n in ("IOTA", "J16", "t1", "CODD", "CEV", "PTa", "PTb", "PTc", "OB", "SELO", "SELA", "SELP", "SEL0", "SEL1", "SEL2",
+           "POS", "BPS", "APS", "VBP", "GA", "GB", "ysb", "nrs"):
+    SCRATCH[_n] = ("sbuf", [128, C], "float32")
+for _n in ("SELD", "SELB", "sc", "upf", "lv", "LS"):
+    SCRATCH[_n] = ("sbuf", [128, C], "bfloat16")
+for _n in ("p16", "p16h", "off", "noff", "thrB", "thr2", "thr3"):
+    SCRATCH[_n] = ("sbuf", [128, 1], "float32")
+for _n in ("C16", "jw", "offi", "offg", "m1", "m2", "m3", "posw", "af", "dpos"):
+    SCRATCH[_n] = ("sbuf", [128, W16], "float32")
+for _n in ("l16", "La", "Lb", "slw", "p2u", "ow", "aw"):
+    SCRATCH[_n] = ("sbuf", [128, W16], "uint16")
 for _k in range(1, ROUNDS + 2):
     SCRATCH["xq%d" % _k] = ("sbuf", [128, C], F8)
     SCRATCH["xs%d" % _k] = ("sbuf", [128, C], "uint8")
 for _k in range(1, ROUNDS + 1):
     SCRATCH["lq%d" % _k] = ("sbuf", [128, C], F8)
     SCRATCH["ls%d" % _k] = ("sbuf", [128, C], "uint8")
-    SCRATCH["abw%d" % _k] = ("sbuf", [128, 2 * W16], "uint16")
-    SCRATCH["lab%d" % _k] = ("sbuf", [128, 2 * W16], "uint16")
-    SCRATCH["lnx%d" % _k] = ("sbuf", [128, 2 * W16], "uint16")
+    for _n in ("abw", "lab", "lnx"):
+        SCRATCH[_n + str(_k)] = ("sbuf", [128, 2 * W16], "uint16")
 
-LOADS = ["nx", "x", "u", "ws", "wc", "v", "y0", "y1", "nr", "oc", "osc0", "osc1", "osc2", "osc3"]
-SEMAPHORES = ["cv", "cs", "ct", "cg"] + ["d_" + n for n in LOADS]
-REMOTE = ["nx"] + [n + str(k) for k in (1, 2, 3) for n in ("q", "s", "ab", "nx")]
-SEMAPHORES += ["r_" + n for n in REMOTE] + ["l_" + n for n in REMOTE]
+LOCAL = ["nx", "x", "u", "ws", "wc", "v", "y0", "y1", "nr", "oc0", "oc1", "osc0", "osc1", "osc2", "osc3"]
+REMOTE = ["nx", "nx2", "nx3", "ab1", "ab2", "ab3"] + [n + str(k) + str(c) for k in (1, 2, 3) for n in "qs" for c in (0, 1)]
+SEMAPHORES = ["cv", "cs", "ct", "cg"] + ["d_" + n for n in LOCAL] + ["r_" + n for n in REMOTE] + ["l_" + n for n in REMOTE]
 
 
 def rank_program(g, core, T, topo):
@@ -95,7 +77,7 @@ def rank_program(g, core, T, topo):
         need = []
         for k in rd:
             need += [e[2] for e in conflicts(writes, k)]
-            if k[0][0] == "P" and k[0] in ("PA", "PB", "PS"):
+            if k[0] in ("PA", "PB", "PS"):
                 need += [e[2] for e in conflicts(reads, k) if e[2][3] != q]
         for k in wr:
             need += [e[2] for e in conflicts(writes, k)]
@@ -120,12 +102,9 @@ def rank_program(g, core, T, topo):
         clock[sem] = total[sem]
         ev = (sem, total[sem], clock, q)
         for k in wr:
-            old = []
-            for e in writes.get(k[0], []):
-                if not (k[1] <= e[0] and e[1] <= k[2]):
-                    old.append(e)
-            writes[k[0]] = old + [(k[1], k[2], ev)]
-            reads[k[0]] = [e for e in reads.get(k[0], []) if not (k[1] <= e[0] and e[1] <= k[2])]
+            for t in (writes, reads):
+                t[k[0]] = [e for e in t.get(k[0], []) if not (k[1] <= e[0] and e[1] <= k[2])]
+            writes[k[0]].append((k[1], k[2], ev))
         for k in rd:
             reads[k[0]] = reads.get(k[0], []) + [(k[1], k[2], ev)]
 
@@ -149,15 +128,16 @@ def rank_program(g, core, T, topo):
         g.remote_dma(out, in_, T.sem["r_" + name], T.sem["l_" + name], pid, rid, topo.mask(core, dst))
         note("g", "l_" + name, len(topo.engines(core, dst)), [norm(rd)], [])
 
-    def arrives(name, src, buf):
+    def arrives(name, src, buf, lo=0, hi=1 << 20):
         n = len(topo.engines(src, core))
         total["r_" + name] = n
-        writes[buf] = [(0, 1 << 20, ("r_" + name, n, {"r_" + name: n}, "x"))]
+        writes[buf] = writes.get(buf, []) + [(lo, hi, ("r_" + name, n, {"r_" + name: n}, "x"))]
 
     partner = [T.cores[rank ^ m] for m in MASKS]
     for k in (1, 2, 3):
-        arrives("q%d" % k, partner[k - 1], "lq%d" % k)
-        arrives("s%d" % k, partner[k - 1], "ls%d" % k)
+        for c, (lo, hi) in enumerate(CH):
+            arrives("q%d%d" % (k, c), partner[k - 1], "lq%d" % k, lo, hi)
+            arrives("s%d%d" % (k, c), partner[k - 1], "ls%d" % k, lo, hi)
         arrives("ab%d" % k, partner[k - 1], "lab%d" % k)
     arrives("nx", partner[0], "lnxi")
     for k in (2, 3):
@@ -177,33 +157,35 @@ def rank_program(g, core, T, topo):
     def vcopy(out, in_, rd, wr):
         op("v", lambda: V.tensor_copy(out, in_), rd, wr)
 
+    def fill(ap, val, wr):
+        op("v", lambda: V.memset(ap, val), [], wr)
+
     def scan(out, d0, d1, init, o0, o1, rd, wr):
         op("v", lambda: V.tensor_tensor_scan(out, d0, d1, init, o0, o1), rd, wr)
 
-    def act(out, in_, rd, wr, scale=1.0, bias=0.0):
-        if bias != 0.0:
-            op("s", lambda: S.activation(out, in_, AF.Identity, bias=bias, scale=scale), rd, wr)
-        elif scale != 1.0:
-            op("s", lambda: S.activation(out, in_, AF.Copy, scale=scale), rd, wr)
-        else:
+    def keep16(out, src, rd, wr):
+        n = out.shape[1]
+        scan(out, T.SELD[:, 0:n], src, 0.0, A.add, A.max, ["SELD"] + rd, wr)
+
+    def act(out, in_, rd, wr, scale=None):
+        if scale is None:
             op("s", lambda: S.activation(out, in_, AF.Copy), rd, wr)
+        else:
+            op("s", lambda: S.activation(out, in_, AF.Copy, scale=scale), rd, wr)
 
-    def quant(codes, plane, tile, lo, hi, key, at=None):
-        src = T[tile][:, 4 * lo:4 * hi] if at is None else T[tile][:, at:at + 4 * (hi - lo)]
-        op("v", lambda: V.quantize_mx(T[codes][:, lo:hi], T[plane][:, lo:hi], src),
-           [key], [(codes, lo, hi), (plane, lo, hi)])
+    def sid(out, in_, rd, wr, scale, bias):
+        op("s", lambda: S.activation(out, in_, AF.Identity, bias=bias, scale=scale), rd, wr)
 
-    def mm(out, pkey, l, ls, a, r, rs, lo, hi):
-        op("t", lambda: g.tensor.matmul_mx(out, T[l][:, a:a + 128], T[ls][:, a:a + 128], T[r][:, lo:hi], T[rs][:, lo:hi], True, True),
-           [(l, a, a + 128), (ls, a, a + 128), (r, lo, hi), (rs, lo, hi)], [pkey])
+    def quant(codes, plane, lo, hi, src, rd):
+        op("v", lambda: V.quantize_mx(T[codes][:, lo:hi], T[plane][:, lo:hi], src), rd, [(codes, lo, hi), (plane, lo, hi)])
 
-    rot = [0]
+    def mm(P, s, n, l, ls, a, r, rs, lo, hi):
+        op("t", lambda: g.tensor.matmul_mx(T[P][:, 512 * s:512 * s + n], T[l][:, a:a + 128], T[ls][:, a:a + 128],
+                                           T[r][:, lo:hi], T[rs][:, lo:hi], True, True),
+           [(l, a, a + 128), (ls, a, a + 128), (r, lo, hi), (rs, lo, hi)], [(P, 512 * s, 512 * s + 512)])
 
-    def sel(src, key):
-        n = "SEL%d" % (rot[0] % 3)
-        rot[0] += 1
-        scan(T[n][:], T.SELD[:], src, 0.0, A.add, A.max, ["SELD", key], [n])
-        return T[n][:, 15:C:16], n
+    def bank(P, s, n):
+        return T[P][:, 512 * s:512 * s + n], (P, 512 * s, 512 * s + 512)
 
     dma("y", "nx", T.nxi[:], T.nx[:], [], ["nxi"])
     dma("s", "x", T.X0[:], T.x[:], [], ["X0"])
@@ -212,206 +194,246 @@ def rank_program(g, core, T, topo):
     dma("y", "wc", T.wq[:].bitcast(dt.uint8), T.wc[:], [], ["wq"])
     dma("y", "v", T.vt[:], T.v[:], [], ["vt"])
 
-    def iota(name, pattern, base, mult, exact=True):
-        if exact:
-            op("g", lambda: g.iota(T[name][:], pattern, base, mult), [], [name])
-        else:
-            op("g", lambda: g.iota(T[name][:], pattern, base, mult, allow_small_or_imprecise_dtypes=True), [], [name])
+    def iota(name, pattern):
+        op("g", lambda: g.iota(T[name][:], pattern, 0, 0, allow_small_or_imprecise_dtypes=True), [], [name])
 
-    iota("pi", [[0, 1]], 0, 1)
-    iota("J16", [[0, W16], [1, 16]], 0, 0, False)
-    iota("IOTA", [[1, C]], 0, 0, False)
-    iota("C16", [[16, W16]], 0, 0, False)
+    op("g", lambda: g.iota(T.pi[:], [[0, 1]], 0, 1), [], ["pi"])
+    iota("J16", [[0, W16], [1, 16]])
+    iota("IOTA", [[1, C]])
+    iota("C16", [[16, W16]])
     send("nx", partner[0], T.lnxi[:], T.nxi[:], "nxi")
 
     ts(T.pj[:], T.pi[:], 15, None, A.bitwise_and, None, ["pi"], ["pj"])
-    op("v", lambda: V.memset(T.ONES[:], 1.0), [], ["ONES"])
+    fill(T.ONES[:], 1.0, ["ONES"])
     ts(T.p16h[:], T.pj[:], 0.5, None, A.add, None, ["pj"], ["p16h"])
     ts(T.p16[:], T.pj[:], 0.0, None, A.add, None, ["pj"], ["p16"])
     ts(T.t1[:], T.J16[:], T.p16h[:, 0:1], 2.0 ** 26, A.subtract, A.mult, ["J16", "p16h"], ["t1"])
     ts(T.off[:], T.p16[:], -K, 15.0 * K, A.mult, A.add, ["p16"], ["off"])
     ts(T.SELD[:], T.t1[:], K, None, A.min, None, ["t1"], ["SELD"])
     vcopy(T.La[:], T.nxi[:], ["nxi"], ["La"])
-    op("v", lambda: V.memset(T.ow[:], 0), [], ["ow"])
-    op("v", lambda: V.memset(T.OB[:, 0:1], 0.0), [], ["OB"])
+    fill(T.ow[:], 0, ["ow"])
+    fill(T.OB[:, 0:1], 0.0, [("OB", 0, 1)])
     op("g", lambda: g.affine_select(T.EB[:], T.ONES[:, 0:516], [[1, 516]], A.is_equal, 0.0, -4, -4), ["ONES"], ["EB"])
 
-    def consts():
-        ts(T.noff[:], T.off[:], -1.0, None, A.mult, None, ["off"], ["noff"])
-        ts(T.jw[:], T.C16[:], T.p16[:, 0:1], None, A.add, None, ["C16", "p16"], ["jw"])
-        ts(T.thrB[:], T.off[:], 2.0 ** -19, 0.5, A.mult, A.add, ["off"], ["thrB"])
-        ts(T.thr2[:], T.off[:], 400000.0, None, A.add, None, ["off"], ["thr2"])
-        ts(T.thr3[:], T.off[:], 600000.0, None, A.subtract, None, ["off"], ["thr3"])
-        ts(T.offi[:], T.jw[:], 1024.0, T.off[:, 0:1], A.mult, A.add, ["jw", "off"], ["offi"])
+    def table(i):
+        if i == 1:
+            sid(T.jw[:], T.C16[:], ["C16", "p16"], ["jw"], 1.0, T.p16[:, 0:1])
+            sid(T.offi[:], T.jw[:], ["jw", "off"], ["offi"], 1024.0, T.off[:, 0:1])
+        if i == 2:
+            sid(T.CODD[:], T.IOTA[:], ["IOTA"], ["CODD"], 1024.0, 512.0)
+        if i == 3:
+            act(T.CEV[:], T.IOTA[:], ["IOTA"], ["CEV"], scale=1024.0)
+        if i == 4:
+            sid(T.offg[:], T.offi[:], ["offi"], ["offg"], 1.0, 512.0)
+            sid(T.noff[:], T.off[:], ["off"], ["noff"], -1.0, 0.0)
+        if i == 7:
+            sid(T.thrB[:], T.off[:], ["off"], ["thrB"], 2.0 ** -19, 0.5)
+            sid(T.thr2[:], T.off[:], ["off"], ["thr2"], 1.0, 400000.0)
+            sid(T.thr3[:], T.off[:], ["off"], ["thr3"], 1.0, -600000.0)
+            act(T.SELB[:], T.SELD[:], ["SELD"], ["SELB"], scale=2.0 ** -19)
+            sid(T.FS[:, 0:1], T.p16[:], ["p16"], [("FS", 0, 1)], 0.0, -float(2 ** 20))
+            sid(T.RS[:, 2 * C + 7:2 * C + 8], T.p16[:], ["p16"], [("RS", 2 * C + 7, 2 * C + 8)], 0.0, float(2 ** 19))
+
+    def ucols():
         vcopy(T.l16[:], T.C16[:], ["C16"], ["l16"])
-        ts(T.offg[:], T.offi[:], 512.0, None, A.add, None, ["offi"], ["offg"])
-        op("v", lambda: V.memset(T.FS[:, 0:1], -float(2 ** 20)), [], [("FS", 0, 1)])
-        op("v", lambda: V.memset(T.RS[:, 2 * C + 7:2 * C + 8], float(2 ** 19)), [], [("RS", 2 * C + 7, 2 * C + 8)])
-
-    def tables():
-        act(T.SELB[:], T.SELD[:], ["SELD"], ["SELB"], scale=2.0 ** -19)
-        act(T.CODD[:], T.IOTA[:], ["IOTA"], ["CODD"], scale=1024.0, bias=512.0)
-        act(T.CEV[:], T.IOTA[:], ["IOTA"], ["CEV"], scale=1024.0)
-
-    def tiles():
-        quant("uq", "uqs", "ut", 0, 128, "ut")
+        quant("uq", "uqs", 0, 128, T.ut[:], ["ut"])
         vcopy(T.up16[:, 0:128].bitcast(dt.uint32), T.uq[:, 0:128].bitcast(dt.uint32).indirect(T.l16[:, 0:8]), ["uq", "l16"], ["up16"])
         act(T.up16s[:, 0:128], T.uqs[:, 0:128].indirect(T.l16[:, 0:8]), ["uqs", "l16"], ["up16s"])
+
+    def etiles():
         for b in range(4):
-            quant("eq", "eqs", "EB", 128 * b, 128 * b + 128, "EB", at=4 - b)
+            quant("eq", "eqs", 128 * b, 128 * b + 128, T.EB[:, 4 - b:516 - b], ["EB"])
 
-    def front(k, c, tile):
+    def scores(k, c):
         lo, hi = CH[c]
-        quant("xq%d" % k, "xs%d" % k, tile, lo, hi, (tile, 4 * lo, 4 * hi))
-        if k <= ROUNDS:
-            mm(T.PS[:, 512 * c:512 * c + hi - lo], ("PS", 512 * c, 512 * c + 512), "up16", "up16s", 0, "xq%d" % k, "xs%d" % k, lo, hi)
+        mm("PS", c, hi - lo, "up16", "up16s", 0, "xq%d" % k, "xs%d" % k, lo, hi)
 
-    def ship(k):
-        p = partner[k - 1]
-        send("q%d" % k, p, T["lq%d" % k][:].bitcast(dt.uint8), T["xq%d" % k][:].bitcast(dt.uint8), "xq%d" % k)
-        send("s%d" % k, p, T["ls%d" % k][:], T["xs%d" % k][:], "xs%d" % k)
+    def ship(k, c):
+        p, (lo, hi) = partner[k - 1], CH[c]
+        send("q%d%d" % (k, c), p, T["lq%d" % k][:, lo:hi].bitcast(dt.uint8), T["xq%d" % k][:, lo:hi].bitcast(dt.uint8), ("xq%d" % k, lo, hi))
+        send("s%d%d" % (k, c), p, T["ls%d" % k][:, lo:hi], T["xs%d" % k][:, lo:hi], ("xs%d" % k, lo, hi))
 
     def signs():
         for c, (lo, hi) in enumerate(CH):
-            op("s", lambda: S.activation(T.sc[:, lo:hi], T.PS[:, 512 * c:512 * c + hi - lo], AF.Sign),
-               [("PS", 512 * c, 512 * c + 512)], [("sc", lo, hi)])
+            src, key = bank("PS", c, hi - lo)
+            op("s", lambda: S.activation(T.sc[:, lo:hi], src, AF.Sign), [key], [("sc", lo, hi)])
             ts(T.upf[:, lo:hi], T.sc[:, lo:hi], 0.0, None, A.max, None, [("sc", lo, hi)], [("upf", lo, hi)])
 
     def unpack(k):
         for b in range(4):
-            mm(T.PA[:, 512 * b:512 * b + C], ("PA", 512 * b, 512 * b + 512), "eq", "eqs", 128 * b, "xq%d" % k, "xs%d" % k, 0, C)
+            mm("PA", b, C, "eq", "eqs", 128 * b, "xq%d" % k, "xs%d" % k, 0, C)
 
     def keep(b):
-        act(T.TH[:, C * b:C * b + C], T.PA[:, 512 * b:512 * b + C], [("PA", 512 * b, 512 * b + 512)], [("TH", C * b, C * b + C)], scale=0.5)
+        src, key = bank("PA", b, C)
+        act(T.TH[:, C * b:C * b + C], src, [key], [("TH", C * b, C * b + C)], scale=0.5)
 
     def unpack_far(k, b):
-        s = b % 2
-        mm(T.PB[:, 512 * s:512 * s + C], ("PB", 512 * s, 512 * s + 512), "eq", "eqs", 128 * b, "lq%d" % k, "ls%d" % k, 0, C)
-        act(T.THP[:, C * b:C * b + C], T.PB[:, 512 * s:512 * s + C], [("PB", 512 * s, 512 * s + 512)], [("THP", C * b, C * b + C)], scale=0.5)
+        src, key = bank("PB", b % 2, C)
+        mm("PB", b % 2, C, "eq", "eqs", 128 * b, "lq%d" % k, "ls%d" % k, 0, C)
+        act(T.THP[:, C * b:C * b + C], src, [key], [("THP", C * b, C * b + C)], scale=0.5)
 
     def places():
-        scan(T.SELP[:], T.SELD[:], T.POS[:], 0.0, A.add, A.max, ["SELD", "POS"], ["SELP"])
-        op("s", lambda: S.activation(T.posw[:], T.SELP[:, 15:C:16], AF.Identity, bias=T.noff[:, 0:1]), ["SELP", "noff"], ["posw"])
+        keep16(T.SELP[:], T.POS[:], ["POS"], ["SELP"])
+        sid(T.posw[:], T.SELP[:, 15:C:16], ["SELP", "noff"], ["posw"], 1.0, T.noff[:, 0:1])
 
     def lay_order():
-        tt(T.VAL[:], T.POS[:], T.IOTA[:], A.add, ["POS", "IOTA"], ["VAL"])
-        ts(T.p2u[:], T.SELP[:, 15:C:16], T.off[:, 0:1], 2.0 ** -9, A.subtract, A.mult, ["SELP", "off"], ["p2u"])
-        op("v", lambda: V.tensor_copy(T.RC[:].indirect(T.p2u[:]), T.VAL[:]), ["VAL", "p2u"], ["RC"])
-
-    def columns_in_order():
-        src, key = sel(T.RC[:, 0:2 * C:2], "RC")
-        tt(T.of[:], src, T.offi[:], A.subtract, [key, "offi"], ["of"])
-        vcopy(T.ow[:], T.of[:], ["of"], ["ow"])
+        ts(T.p2u[:], T.SELP[:, 15:C:16], T.off[:, 0:1], 2.0 ** -10, A.subtract, A.mult, ["SELP", "off"], ["p2u"])
+        op("v", lambda: V.tensor_copy(T.OB[:].indirect(T.p2u[:]), T.IOTA[:]), ["IOTA", "p2u"], ["OB"])
 
     def far_ring(lst, key):
         act(T.APS[:], T.IOTA[:].indirect(T[lst][:, 0:W16]), ["IOTA", key], ["APS"])
 
-    def far_places(lst, key):
-        act(T.VBP[:], T.POS[:].indirect(T[lst][:, W16:2 * W16]), ["POS", key], ["VBP"], bias=512.0)
+    def far_places(lst):
+        sid(T.VBP[:], T.POS[:].indirect(T[lst][:, W16:2 * W16]), ["POS", lst], ["VBP"], 1.0, 512.0)
 
-    def guests():
-        tt(T.RC[:, 1:2 * C:2], T.APS[:].indirect(T.ow[:]), T.CODD[:], A.add, ["APS", "ow", "CODD"], ["RC"])
-        src, key = sel(T.RC[:, 1:2 * C:2], "RC")
-        tt(T.af[:], src, T.offg[:], A.subtract, [key, "offg"], ["af"])
+    def guests(lo, hi):
+        tt(T.RC[:, 1 + 2 * lo:2 * hi:2], T.APS[:].indirect(T.ow[:, lo // 16:hi // 16]), T.CODD[:, lo:hi], A.add,
+           ["APS", ("ow", lo, hi), "CODD"], [("RCO", lo, hi)])
+
+    def evens(lo, hi):
+        tt(T.RC[:, 2 * lo:2 * hi:2], T.OB[:, lo:hi], T.CEV[:, lo:hi], A.add, [("OB", lo, hi), "CEV"], [("RCE", lo, hi)])
+
+    def guest_scan(lo, hi):
+        keep16(T.SELA[:, lo:hi], T.RC[:, 1 + 2 * lo:2 * hi:2], [("RCO", lo, hi)], [("SELA", lo, hi)])
+
+    def guest_cols():
+        tt(T.af[:], T.SELA[:, 15:C:16], T.offg[:], A.subtract, ["SELA", "offg"], ["af"])
+
+    def guest_list():
         vcopy(T.aw[:], T.af[:], ["af"], ["aw"])
 
     def hosts():
-        src, key = sel(T.VBP[:], "VBP")
-        tt(T.dpos[:], src, T.SELP[:, 15:C:16], A.subtract, [key, "SELP"], ["dpos"])
+        keep16(T.SEL0[:], T.VBP[:], ["VBP"], ["SEL0"])
+        tt(T.dpos[:], T.SEL0[:, 15:C:16], T.SELP[:, 15:C:16], A.subtract, ["SEL0", "SELP"], ["dpos"])
 
     def negatives():
-        act(T.NC[:], T.RC[:], ["RC"], ["NC"], bias=-float(2 ** 19))
+        sid(T.NC[:], T.RC[:], ["RCE", "RCO"], ["NC"], 1.0, -float(2 ** 19))
 
-    def splice(k, lst, key):
-        tt(T.lv[:], T.upf[:].indirect(T[lst][:, W16:2 * W16]), T.sc[:], A.is_lt, ["upf", "sc", key], ["lv"])
-        keep(0)
-        keep(1)
+    def splice(k):
+        lst, abw = "lnx%d" % k, "abw%d" % k
+        h = W16
+        tt(T.lv[:], T.upf[:].indirect(T[lst][:, h:2 * h]), T.sc[:], A.is_lt, ["upf", "sc", lst], ["lv"])
+        if k > 1:
+            keep(0)
+            keep(1)
         act(T.inv[:, 0:2 * C:2], T.lv[:].indirect(T.ow[:]), ["lv", "ow"], ["inve"])
-        act(T.inv[:, 1 + 2 * GS:2 * C:2], T.lv[:].indirect(T.aw[:, GS // 16:W16]), ["lv", "aw"], ["invp"], scale=-1.0, bias=1.0)
-        ts(T.inv[:, 1:2 * GS:2], T.lv[:].indirect(T.aw[:, 0:GS // 16]), -1.0, 1.0, A.mult, A.add, ["lv", "aw"], ["invo"])
+        sid(T.inv[:, 1 + 2 * GS:2 * C:2], T.lv[:].indirect(T.aw[:, GS // 16:h]), ["lv", "aw"], ["invp"], -1.0, 1.0)
         scan(T.LS[:], T.SELB[:], T.lv[:], 0.0, A.add, A.max, ["SELB", "lv"], ["LS"])
+        ts(T.inv[:, 1:2 * GS:2], T.lv[:].indirect(T.aw[:, 0:GS // 16]), -1.0, 1.0, A.mult, A.add, ["lv", "aw"], ["invo"])
         ts(T.m1[:], T.LS[:, 15:C:16], T.thrB[:, 0:1], None, A.is_ge, None, ["LS", "thrB"], ["m1"])
         tt(T.m2[:], T.m1[:], T.dpos[:], A.mult, ["m1", "dpos"], ["m2"])
         tt(T.m3[:], T.m2[:], T.posw[:], A.add, ["m2", "posw"], ["m3"])
         ts(T.slw[:], T.m3[:], 2.0 ** -9, None, A.mult, None, ["m3"], ["slw"])
-        keep(2)
-        keep(3)
-        scan(T.FS[:, 1:2 * C + 1], T.inv[:], T.NC[:], -float(2 ** 20), A.mult, A.min, ["inve", "invo", "invp", "NC"], [("FS", 1, 2 * C + 8)])
+        if k > 1:
+            keep(2)
+            keep(3)
+        void = ["inve", "invo", "invp"]
+        scan(T.FS[:, 1:2 * C + 1], T.inv[:], T.NC[:], -float(2 ** 20), A.mult, A.min, void + ["NC"], [("FS", 1, 2 * C + 8)])
         act(T.GB[:], T.FS[:, 0:2 * C].indirect(T.slw[:]), ["FS", "slw"], ["GB"])
         scan(T.RS[:, 2 * C + 6:6:-1], T.inv[:, ::-1], T.RC[:, ::-1], float(2 ** 19), A.mult, A.max,
-             ["inve", "invo", "invp", "RC"], [("RS", 0, 2 * C + 7)])
+             void + ["RCE", "RCO"], [("RS", 0, 2 * C + 7)])
         act(T.GA[:], T.RS[:, 8:2 * C + 8].indirect(T.slw[:]), ["RS", "slw"], ["GA"])
-        sb, kb = sel(T.GB[:], "GB")
-        op("s", lambda: S.activation(T.cab[:, W16:2 * W16], sb, AF.Identity, bias=T.noff[:, 0:1]), [kb, "noff"], [("cab", W16, 2 * W16)])
-        ts(T.tab[:, W16:2 * W16], sb, T.thr3[:, 0:1], T.FS[:, 2 * C:2 * C + 1], A.is_le, A.mult, [kb, "thr3", "FS"], [("tab", W16, 2 * W16)])
-        sa, ka = sel(T.GA[:], "GA")
-        op("s", lambda: S.activation(T.cab[:, 0:W16], sa, AF.Identity, bias=T.noff[:, 0:1]), [ka, "noff"], [("cab", 0, W16)])
-        ts(T.tab[:, 0:W16], sa, T.thr2[:, 0:1], T.RS[:, 7:8], A.is_ge, A.mult, [ka, "thr2", "RS"], [("tab", 0, W16)])
+        keep16(T.SEL1[:], T.GB[:], ["GB"], ["SEL1"])
+        sid(T.cab[:, h:2 * h], T.SEL1[:, 15:C:16], ["SEL1", "noff"], [("cab", h, 2 * h)], 1.0, T.noff[:, 0:1])
+        keep16(T.SEL2[:], T.GA[:], ["GA"], ["SEL2"])
+        sid(T.cab[:, 0:h], T.SEL2[:, 15:C:16], ["SEL2", "noff"], [("cab", 0, h)], 1.0, T.noff[:, 0:1])
+        ts(T.tab[:, h:2 * h], T.SEL1[:, 15:C:16], T.thr3[:, 0:1], T.FS[:, 2 * C:2 * C + 1], A.is_le, A.mult, ["SEL1", "thr3", "FS"], [("tab", h, 2 * h)])
+        ts(T.tab[:, 0:h], T.SEL2[:, 15:C:16], T.thr2[:, 0:1], T.RS[:, 7:8], A.is_ge, A.mult, ["SEL2", "thr2", "RS"], [("tab", 0, h)])
         tt(T.iab[:], T.cab[:], T.tab[:], A.add, ["cab", "tab"], ["iab"])
         ts(T.jab[:], T.iab[:], 511, None, A.bitwise_and, None, ["iab"], ["jab"])
-        abw = "abw%d" % k
         vcopy(T[abw][:], T.jab[:], ["jab"], [abw])
         send("ab%d" % k, partner[k - 1], T["lab%d" % k][:], T[abw][:], abw)
         if k < ROUNDS:
             send("nx%d" % (k + 1), partner[k], T["lnx%d" % (k + 1)][:], T[abw][:], abw)
 
-    def jump(out, win, lst):
-        act(T[out][:, PS_:C], T[win][:].indirect(T[lst][:, PS_ // 16:W16]), [win, lst], [(out, PS_, C)])
-        vcopy(T[out][:, 0:PS_], T[win][:].indirect(T[lst][:, 0:PS_ // 16]), [win, lst], [(out, 0, PS_)])
+    def jump(out, win, lst, share):
+        for lo, hi in CH0[::-1] if share else CH0:
+            (vcopy if share and lo == 0 else act)(T[out][:, lo:hi], T[win][:].indirect(T[lst][:, lo // 16:hi // 16]), [win, lst], [(out, lo, hi)])
 
-    jump("PTa", "IOTA", "La")
-    for i in range(9):
+    def ahead(P, m, n, a):
+        b = 0 if m < 16 else m
+        act(T.OB[:, m:m + n], T[P][:].indirect(T.ow[:, a // 16:(a + n) // 16]), [P, ("ow", a, a + n)], [("OB", m, m + n)])
+        keep16(T.SELO[:, b:b + n], T.OB[:, b:b + n], [("OB", b, b + n)], [("SELO", b, b + n)])
+
+    def enlist(m, n):
+        b = 0 if m < 16 else m
+        ts(T.ow[:, b // 16:(b + n) // 16], T.SELO[:, b + 15:b + n:16], T.off[:, 0:1], None, A.subtract, None,
+           [("SELO", b, b + n), "off"], [("ow", b, b + n)])
+
+    jump("PTa", "IOTA", "La", True)
+    for i in range(TOP + 1):
         L, L2 = ("La", "Lb") if i % 2 == 0 else ("Lb", "La")
         P, P2 = (("PTa", "PTb"), ("PTb", "PTc"), ("PTc", "PTa"))[i % 3]
-        m = 2 ** i
-        n = min(max(16, m), C - m)
-        if i < 8:
-            jump(P2, P, L)
-        act(T.OB[:, m:m + n], T[P][:].indirect(T.ow[:, 0:n // 16]), [P, "ow"], ["OB"])
-        if i < 7:
-            src, key = sel(T[P2][:], P2)
-            ts(T[L2][:], src, T.off[:, 0:1], None, A.subtract, None, [key, "off"], [L2])
-        a = 0 if m < 16 else m
-        scan(T.SELO[:, 0:n], T.SELD[:, 0:n], T.OB[:, a:a + n], 0.0, A.add, A.max, ["SELD", "OB"], ["SELO"])
-        ts(T.ow[:, a // 16:(a + n) // 16], T.SELO[:, 15:n:16], T.off[:, 0:1], None, A.subtract, None, ["SELO", "off"], ["ow"])
-        if i == 0:
-            consts()
-            tables()
+        n = "SEL%d" % (i % 3)
+        if i < TOP:
+            jump(P2, P, L, i < 3)
+        if i < TOP - 1:
+            for lo, hi in CH0:
+                keep16(T[n][:, lo:hi], T[P2][:, lo:hi], [(P2, lo, hi)], [(n, lo, hi)])
+        ahead(P, 2 ** i, max(16, 2 ** i), 0)
+        if i < TOP - 1:
+            ts(T[L2][:], T[n][:, 15:C:16], T.off[:, 0:1], None, A.subtract, None, [n, "off"], [L2])
+        enlist(2 ** i, max(16, 2 ** i))
+        table(i)
         if i == 1:
-            tiles()
+            ucols()
         if i == 2:
-            front(1, 0, "X0")
-            front(1, 1, "X0")
-            ship(1)
-            unpack(1)
+            etiles()
         if i == 3:
-            signs()
+            for c, (lo, hi) in enumerate(CH):
+                quant("xq1", "xs1", lo, hi, T.X0[:, 4 * lo:4 * hi], ["X0"])
+                scores(1, c)
+                ship(1, c)
+            unpack(1)
         if i == 4:
             vcopy(T.lnx1[:, 0:W16], T.lnxi[:], ["lnxi"], [("lnx1", 0, W16)])
             op("v", lambda: V.tensor_copy(T.BPS[:].indirect(T.lnx1[:, 0:W16]), T.IOTA[:]), ["IOTA", ("lnx1", 0, W16)], ["BPS"])
-            src, key = sel(T.BPS[:], "BPS")
-            ts(T.lnx1[:, W16:2 * W16], src, T.off[:, 0:1], None, A.subtract, None, [key, "off"], [("lnx1", W16, 2 * W16)])
-        if i == 7:
-            far_ring("lnx1", "lnx1")
+        if i == 5:
+            far_ring("lnx1", ("lnx1", 0, W16))
+            signs()
+            keep16(T.SELA[:], T.BPS[:], ["BPS"], ["SELA"])
+            ts(T.lnx1[:, W16:2 * W16], T.SELA[:, 15:C:16], T.off[:, 0:1], None, A.subtract, None, ["SELA", "off"], [("lnx1", W16, 2 * W16)])
+    far = ("PTa", "PTb", "PTc")[TOP % 3]
+    keep(0)
+    ahead(far, 128, 64, 64)
+    enlist(128, 64)
+    guests(0, 128)
+    keep(1)
+    ahead(far, 192, 64, 128)
+    enlist(192, 64)
+    guest_scan(0, 128)
+    keep(2)
+    ahead(far, 256, 64, 192)
+    enlist(256, 64)
+    evens(0, 192)
+    ahead(far, 320, 32, 256)
+    enlist(320, 32)
+    guests(128, C)
     op("v", lambda: V.tensor_copy(T.POS[:].indirect(T.ow[:]), T.CEV[:]), ["ow", "CEV"], ["POS"])
-    far_places("lnx1", "lnx1")
-    guests()
+    table(7)
+    keep(3)
+    far_places("lnx1")
+    guest_scan(128, C)
     places()
-    tt(T.RC[:, 0:2 * C:2], T.OB[:], T.CEV[:], A.add, ["OB", "CEV"], ["RC"])
+    guest_cols()
+    evens(192, C)
+    guest_list()
     negatives()
     hosts()
 
     for k in range(1, ROUNDS + 1):
-        lst = "lnx%d" % k
+        last = k == ROUNDS
         if k > 1:
             signs()
-        splice(k, lst, lst)
-        abw, lab = "abw%d" % k, "lab%d" % k
+        splice(k)
+        abw, lab, lnx = "abw%d" % k, "lab%d" % k, "lnx%d" % (k + 1)
+        xq, xs = "xq%d" % (k + 1), "xs%d" % (k + 1)
 
-        def own(t, q):
-            (act if q == "s" else vcopy)(T.TB[:, C * t:C * t + C], T.TH[:, C * t:C * t + C].indirect(T[abw][:, W16:2 * W16]),
-                                         [("TH", C * t, C * t + C), abw], [("TB", C * t, C * t + C)])
-        if k < ROUNDS:
+        def own(t, q, lo=0, hi=C):
+            (act if q == "s" else vcopy)(T.TB[:, C * t + lo:C * t + hi],
+                                         T.TH[:, C * t:C * t + C].indirect(T[abw][:, W16 + lo // 16:W16 + hi // 16]),
+                                         [("TH", C * t, C * t + C), abw], [("TB", C * t + lo, C * t + hi)])
+        if not last:
             scan(T.CNT[:], T.ONES[:], T.inv[:], -1.0, A.add, A.subtract, ["ONES", "inve", "invo", "invp"], ["CNT"])
             unpack_far(k, 0)
             act(T.POS[:], T.CNT[:].indirect(T.slw[:]), ["CNT", "slw"], ["POS"], scale=1024.0)
@@ -419,64 +441,71 @@ def rank_program(g, core, T, topo):
             for b in (1, 2, 3):
                 unpack_far(k, b)
             places()
-            lay_order()
             own(1, "v")
-            for t in (2, 3):
-                own(t, "s")
+            lay_order()
+            own(2, "v", 0, 192)
+            own(2, "s", 192, C)
+            own(3, "s")
         else:
             for b in range(4):
                 unpack_far(k, b)
-            quant("vq", "vqs", "vt", 0, 128, "vt")
+            quant("vq", "vqs", 0, 128, T.vt[:], ["vt"])
             for t in range(4):
                 own(t, "v")
         for c, (lo, hi) in enumerate(CH):
             for t in range(4):
-                act(T.TBP[:, C * t + lo:C * t + hi], T.THP[:, C * t:C * t + C].indirect(T[lab][:, W16 + lo // 16:W16 + hi // 16]),
-                    [("THP", C * t, C * t + C), lab], [("TBP", C * t + lo, C * t + hi)])
-                tt(T.Z[:, 4 * lo + t:4 * hi:4], T.THP[:, C * t:C * t + C].indirect(T[lab][:, lo // 16:hi // 16]),
-                   T.TBP[:, C * t + lo:C * t + hi], A.add,
-                   [("THP", C * t, C * t + C), lab, ("TBP", C * t + lo, C * t + hi)], [("Z%d" % t, lo, hi)])
-            op("v", lambda: V.quantize_mx(T.zq[:, lo:hi], T.zqs[:, lo:hi], T.Z[:, 4 * lo:4 * hi]),
-               [("Z%d" % t, lo, hi) for t in range(4)], [("zq", lo, hi), ("zqs", lo, hi)])
-        if k < ROUNDS:
-            far_ring("lnx%d" % (k + 1), "lnx%d" % (k + 1))
-            far_places("lnx%d" % (k + 1), "lnx%d" % (k + 1))
+                W = C * t
+                act(T.TBP[:, W + lo:W + hi], T.THP[:, W:W + C].indirect(T[lab][:, W16 + lo // 16:W16 + hi // 16]),
+                    [("THP", W, W + C), lab], [("TBP", W + lo, W + hi)])
+                tt(T.Z[:, 4 * lo + t:4 * hi:4], T.THP[:, W:W + C].indirect(T[lab][:, lo // 16:hi // 16]), T.TBP[:, W + lo:W + hi], A.add,
+                   [("THP", W, W + C), lab, ("TBP", W + lo, W + hi)], [("Z%d" % t, lo, hi)])
+            quant("zq", "zqs", lo, hi, T.Z[:, 4 * lo:4 * hi], [("Z%d" % t, lo, hi) for t in range(4)])
+        if not last:
+            far_ring(lnx, lnx)
+            far_places(lnx)
         else:
             act(T.nrs[:], T.IOTA[:].indirect(T[abw][:, 0:W16]), ["IOTA", abw], ["nrs"])
             dma("y", "nr", T.nr[:], T.nrs[0:128:16, :], ["nrs"], [])
         for c, (lo, hi) in enumerate(CH):
             for b in range(4):
-                if c == 0:
-                    P, s = "PA", b
+                P, s = ("PA", b) if c == 0 else ("PB", b) if b < 2 else ("PA", b - 2)
+                mm(P, s, hi - lo, "wq", "wsq", 128 * b, "zq", "zqs", lo, hi)
+                src, key = bank(P, s, hi - lo)
+                if last and c == 1 and b % 2:
+                    ts(T.HH[:, C * b + lo:C * b + hi], src, 2.0 ** -6, None, A.mult, None, [key], [("HH", C * b + lo, C * b + hi)])
                 else:
-                    P, s = ("PB", b) if b < 2 else ("PA", b - 2)
-                mm(T[P][:, 512 * s:512 * s + hi - lo], (P, 512 * s, 512 * s + 512), "wq", "wsq", 128 * b, "zq", "zqs", lo, hi)
-                act(T.HH[:, C * b + lo:C * b + hi], T[P][:, 512 * s:512 * s + hi - lo],
-                    [(P, 512 * s, 512 * s + 512)], [("HH", C * b + lo, C * b + hi)], scale=2.0 ** -6)
-        if k < ROUNDS:
-            columns_in_order()
-            guests()
-            hosts()
+                    act(T.HH[:, C * b + lo:C * b + hi], src, [key], [("HH", C * b + lo, C * b + hi)], scale=2.0 ** -6)
+        if not last:
+            keep16(T.SELO[:], T.OB[:], ["OB"], ["SELO"])
+            evens(0, C)
+            ts(T.ow[:], T.SELO[:, 15:C:16], T.off[:, 0:1], None, A.subtract, None, ["SELO", "off"], ["ow"])
+            guests(0, C)
+            guest_scan(0, C)
+            guest_cols()
             negatives()
         for c, (lo, hi) in enumerate(CH):
             for t in range(4):
-                tt(T.X1[:, 4 * lo + t:4 * hi:4], T.HH[:, C * t:C * t + C].indirect(T[abw][:, lo // 16:hi // 16]),
-                   T.TB[:, C * t + lo:C * t + hi], A.add,
-                   [("HH", C * t, C * t + C), abw, ("TB", C * t, C * t + C)], [("X1_%d" % t, 4 * lo, 4 * hi)])
-            op("v", lambda: V.quantize_mx(T["xq%d" % (k + 1)][:, lo:hi], T["xs%d" % (k + 1)][:, lo:hi], T.X1[:, 4 * lo:4 * hi]),
-               [("X1_%d" % t, 4 * lo, 4 * hi) for t in range(4)], [("xq%d" % (k + 1), lo, hi), ("xs%d" % (k + 1), lo, hi)])
-            if k < ROUNDS:
-                mm(T.PS[:, 512 * c:512 * c + hi - lo], ("PS", 512 * c, 512 * c + 512), "up16", "up16s", 0, "xq%d" % (k + 1), "xs%d" % (k + 1), lo, hi)
+                W = C * t
+                tt(T.X1[:, 4 * lo + t:4 * hi:4], T.HH[:, W:W + C].indirect(T[abw][:, lo // 16:hi // 16]), T.TB[:, W + lo:W + hi], A.add,
+                   [("HH", W, W + C), abw, ("TB", W, W + C)], [("X1_%d" % t, lo, hi)])
+                if not last and c == 0 and t == 0:
+                    guest_list()
+            quant(xq, xs, lo, hi, T.X1[:, 4 * lo:4 * hi], [("X1_%d" % t, lo, hi) for t in range(4)])
+            if not last:
+                scores(k + 1, c)
+                ship(k + 1, c)
             else:
-                mm(T.PS[:, 512 * c:512 * c + hi - lo], ("PS", 512 * c, 512 * c + 512), "vq", "vqs", 0, "xq4", "xs4", lo, hi)
-                act(T.ysb[:, lo:hi], T.PS[:, 512 * c:512 * c + hi - lo], [("PS", 512 * c, 512 * c + 512)], [("ysb", lo, hi)])
+                mm("PS", c, hi - lo, "vq", "vqs", 0, xq, xs, lo, hi)
+                dma("y", "oc%d" % c, T.oc[:, 4 * lo:4 * hi], T[xq][:, lo:hi].bitcast(dt.uint8), [(xq, lo, hi)], [])
+                if c == 1:
+                    for i in range(4):
+                        dma("y", "osc%d" % i, T.osc[4 * i:4 * i + 4, :], T[xs][32 * i:32 * i + 4, :], [xs], [])
+                src, key = bank("PS", c, hi - lo)
+                act(T.ysb[:, lo:hi], src, [key], [("ysb", lo, hi)])
                 dma("y", "y%d" % c, T.y[:, lo:hi], T.ysb[:, lo:hi], [("ysb", lo, hi)], [])
-        if k < ROUNDS:
-            ship(k + 1)
+        if not last:
             unpack(k + 1)
-    dma("y", "oc", T.oc[:], T.xq4[:].bitcast(dt.uint8), ["xq4"], [])
-    for i in range(4):
-        dma("y", "osc%d" % i, T.osc[4 * i:4 * i + 4, :], T.xs4[32 * i:32 * i + 4, :], ["xs4"], [])
+            hosts()
     for sem, val in total.items():
         if know["g"].get(sem, 0) < val:
             g.wait_ge(T.sem[sem], val)

@@ -7,7 +7,7 @@ MASKS = [1, 2, 4]
 ROUNDS = 3
 W16 = C // 16
 K = float(2 ** 20)
-GS = 192
+GS = 160
 TOP = 6
 F8 = "float8_e4m3fn_x4"
 
@@ -230,7 +230,6 @@ def rank_program(g, core, T, topo):
             sid(T.thrB[:], T.off[:], ["off"], ["thrB"], 2.0 ** -19, 0.5)
             sid(T.thr2[:], T.off[:], ["off"], ["thr2"], 1.0, 400000.0)
             sid(T.thr3[:], T.off[:], ["off"], ["thr3"], 1.0, -600000.0)
-            act(T.SELB[:], T.SELD[:], ["SELD"], ["SELB"], scale=2.0 ** -19)
             sid(T.FS[:, 0:1], T.p16[:], ["p16"], [("FS", 0, 1)], 0.0, -float(2 ** 20))
             sid(T.RS[:, 2 * C + 7:2 * C + 8], T.p16[:], ["p16"], [("RS", 2 * C + 7, 2 * C + 8)], 0.0, float(2 ** 19))
 
@@ -309,24 +308,33 @@ def rank_program(g, core, T, topo):
     def negatives():
         sid(T.NC[:], T.RC[:], ["RCE", "RCO"], ["NC"], 1.0, -float(2 ** 19))
 
+    def leavers(lst):
+        tt(T.lv[:], T.upf[:].indirect(T[lst][:, W16:2 * W16]), T.sc[:], A.is_lt, ["upf", "sc", lst], ["lv"])
+
+    def void_evens():
+        act(T.inv[:, 0:2 * C:2], T.lv[:].indirect(T.ow[:]), ["lv", "ow"], ["inve"])
+
+    def leaver_bits():
+        scan(T.LS[:], T.SELB[:], T.lv[:], 0.0, A.add, A.max, ["SELB", "lv"], ["LS"])
+
     def splice(k):
         lst, abw = "lnx%d" % k, "abw%d" % k
         h = W16
-        tt(T.lv[:], T.upf[:].indirect(T[lst][:, h:2 * h]), T.sc[:], A.is_lt, ["upf", "sc", lst], ["lv"])
         if k > 1:
+            leavers(lst)
             keep(0)
             keep(1)
-        act(T.inv[:, 0:2 * C:2], T.lv[:].indirect(T.ow[:]), ["lv", "ow"], ["inve"])
+            void_evens()
         sid(T.inv[:, 1 + 2 * GS:2 * C:2], T.lv[:].indirect(T.aw[:, GS // 16:h]), ["lv", "aw"], ["invp"], -1.0, 1.0)
-        scan(T.LS[:], T.SELB[:], T.lv[:], 0.0, A.add, A.max, ["SELB", "lv"], ["LS"])
+        if k > 1:
+            leaver_bits()
         ts(T.inv[:, 1:2 * GS:2], T.lv[:].indirect(T.aw[:, 0:GS // 16]), -1.0, 1.0, A.mult, A.add, ["lv", "aw"], ["invo"])
         ts(T.m1[:], T.LS[:, 15:C:16], T.thrB[:, 0:1], None, A.is_ge, None, ["LS", "thrB"], ["m1"])
         tt(T.m2[:], T.m1[:], T.dpos[:], A.mult, ["m1", "dpos"], ["m2"])
         tt(T.m3[:], T.m2[:], T.posw[:], A.add, ["m2", "posw"], ["m3"])
         ts(T.slw[:], T.m3[:], 2.0 ** -9, None, A.mult, None, ["m3"], ["slw"])
-        if k > 1:
-            keep(2)
-            keep(3)
+        keep(2)
+        keep(3)
         void = ["inve", "invo", "invp"]
         scan(T.FS[:, 1:2 * C + 1], T.inv[:], T.NC[:], -float(2 ** 20), A.mult, A.min, void + ["NC"], [("FS", 1, 2 * C + 8)])
         act(T.GB[:], T.FS[:, 0:2 * C].indirect(T.slw[:]), ["FS", "slw"], ["GB"])
@@ -335,6 +343,10 @@ def rank_program(g, core, T, topo):
         act(T.GA[:], T.RS[:, 8:2 * C + 8].indirect(T.slw[:]), ["RS", "slw"], ["GA"])
         keep16(T.SEL1[:], T.GB[:], ["GB"], ["SEL1"])
         sid(T.cab[:, h:2 * h], T.SEL1[:, 15:C:16], ["SEL1", "noff"], [("cab", h, 2 * h)], 1.0, T.noff[:, 0:1])
+        if k < ROUNDS:
+            scan(T.CNT[:, 0:C], T.ONES[:, 0:C], T.inv[:, 0:C], -1.0, A.add, A.subtract, ["ONES"] + void, [("CNT", 0, C)])
+        else:
+            quant("vq", "vqs", 0, 128, T.vt[:], ["vt"])
         keep16(T.SEL2[:], T.GA[:], ["GA"], ["SEL2"])
         sid(T.cab[:, 0:h], T.SEL2[:, 15:C:16], ["SEL2", "noff"], [("cab", 0, h)], 1.0, T.noff[:, 0:1])
         ts(T.tab[:, h:2 * h], T.SEL1[:, 15:C:16], T.thr3[:, 0:1], T.FS[:, 2 * C:2 * C + 1], A.is_le, A.mult, ["SEL1", "thr3", "FS"], [("tab", h, 2 * h)])
@@ -394,15 +406,16 @@ def rank_program(g, core, T, topo):
             keep16(T.SELA[:], T.BPS[:], ["BPS"], ["SELA"])
             ts(T.lnx1[:, W16:2 * W16], T.SELA[:, 15:C:16], T.off[:, 0:1], None, A.subtract, None, ["SELA", "off"], [("lnx1", W16, 2 * W16)])
     far = ("PTa", "PTb", "PTc")[TOP % 3]
-    keep(0)
+    leavers("lnx1")
     ahead(far, 128, 64, 64)
     enlist(128, 64)
     guests(0, 128)
-    keep(1)
+    act(T.SELB[:], T.SELD[:], ["SELD"], ["SELB"], scale=2.0 ** -19)
     ahead(far, 192, 64, 128)
     enlist(192, 64)
     guest_scan(0, 128)
-    keep(2)
+    keep(0)
+    leaver_bits()
     ahead(far, 256, 64, 192)
     enlist(256, 64)
     evens(0, 192)
@@ -410,8 +423,9 @@ def rank_program(g, core, T, topo):
     enlist(320, 32)
     guests(128, C)
     op("v", lambda: V.tensor_copy(T.POS[:].indirect(T.ow[:]), T.CEV[:]), ["ow", "CEV"], ["POS"])
+    void_evens()
     table(7)
-    keep(3)
+    keep(1)
     far_places("lnx1")
     guest_scan(128, C)
     places()
@@ -434,22 +448,22 @@ def rank_program(g, core, T, topo):
                                          T.TH[:, C * t:C * t + C].indirect(T[abw][:, W16 + lo // 16:W16 + hi // 16]),
                                          [("TH", C * t, C * t + C), abw], [("TB", C * t + lo, C * t + hi)])
         if not last:
-            scan(T.CNT[:], T.ONES[:], T.inv[:], -1.0, A.add, A.subtract, ["ONES", "inve", "invo", "invp"], ["CNT"])
+            scan(T.CNT[:, C:2 * C], T.ONES[:, C:2 * C], T.inv[:, C:2 * C], T.CNT[:, C - 1:C], A.add, A.subtract,
+                 ["ONES", "inve", "invo", "invp", ("CNT", 0, C)], [("CNT", C, 2 * C)])
             unpack_far(k, 0)
             act(T.POS[:], T.CNT[:].indirect(T.slw[:]), ["CNT", "slw"], ["POS"], scale=1024.0)
             own(0, "v")
             for b in (1, 2, 3):
                 unpack_far(k, b)
             places()
-            own(1, "v")
+            own(1, "s")
             lay_order()
-            own(2, "v", 0, 192)
-            own(2, "s", 192, C)
-            own(3, "s")
+            keep16(T.SELO[:], T.OB[:], ["OB"], ["SELO"])
+            evens(0, C)
+            ts(T.ow[:], T.SELO[:, 15:C:16], T.off[:, 0:1], None, A.subtract, None, ["SELO", "off"], ["ow"])
         else:
             for b in range(4):
                 unpack_far(k, b)
-            quant("vq", "vqs", 0, 128, T.vt[:], ["vt"])
             for t in range(4):
                 own(t, "v")
         for c, (lo, hi) in enumerate(CH):
@@ -462,7 +476,6 @@ def rank_program(g, core, T, topo):
             quant("zq", "zqs", lo, hi, T.Z[:, 4 * lo:4 * hi], [("Z%d" % t, lo, hi) for t in range(4)])
         if not last:
             far_ring(lnx, lnx)
-            far_places(lnx)
         else:
             act(T.nrs[:], T.IOTA[:].indirect(T[abw][:, 0:W16]), ["IOTA", abw], ["nrs"])
             dma("y", "nr", T.nr[:], T.nrs[0:128:16, :], ["nrs"], [])
@@ -476,18 +489,19 @@ def rank_program(g, core, T, topo):
                 else:
                     act(T.HH[:, C * b + lo:C * b + hi], src, [key], [("HH", C * b + lo, C * b + hi)], scale=2.0 ** -6)
         if not last:
-            keep16(T.SELO[:], T.OB[:], ["OB"], ["SELO"])
-            evens(0, C)
-            ts(T.ow[:], T.SELO[:, 15:C:16], T.off[:, 0:1], None, A.subtract, None, ["SELO", "off"], ["ow"])
             guests(0, C)
             guest_scan(0, C)
             guest_cols()
+            for lo, hi in CH:
+                for t in (2, 3):
+                    own(t, "s", lo, hi)
+            far_places(lnx)
             negatives()
         for c, (lo, hi) in enumerate(CH):
             for t in range(4):
                 W = C * t
                 tt(T.X1[:, 4 * lo + t:4 * hi:4], T.HH[:, W:W + C].indirect(T[abw][:, lo // 16:hi // 16]), T.TB[:, W + lo:W + hi], A.add,
-                   [("HH", W, W + C), abw, ("TB", W, W + C)], [("X1_%d" % t, lo, hi)])
+                   [("HH", W, W + C), abw, ("TB", W + lo, W + hi)], [("X1_%d" % t, lo, hi)])
                 if not last and c == 0 and t == 0:
                     guest_list()
             quant(xq, xs, lo, hi, T.X1[:, 4 * lo:4 * hi], [("X1_%d" % t, lo, hi) for t in range(4)])

from concourse.mybir import dt, AluOpType, ActivationFunctionType

C = 352
CH = [(0, 224), (224, 352)]
CH0 = [(0, 192), (192, 352)]
MASKS = [1, 2, 4]
ROUNDS = 3
W16 = C // 16
K = float(2 ** 20)
GS = 160
TOP = 6
F8 = "float8_e4m3fn_x4"

SCRATCH = {
    "nxi": ("sbuf", [128, W16], "int32"), "lnxi": ("sbuf", [128, W16], "int32"),
    "ut": ("sbuf", [128, 512], "bfloat16"), "vt": ("sbuf", [128, 512], "bfloat16"),
    "wq": ("sbuf", [128, 512], F8), "wsq": ("sbuf", [128, 512], "uint8"),
    "uq": ("sbuf", [128, 128], F8), "uqs": ("sbuf", [128, 128], "uint8"),
    "up16": ("sbuf", [128, 128], F8), "up16s": ("sbuf", [128, 128], "uint8"),
    "vq": ("sbuf", [128, 128], F8), "vqs": ("sbuf", [128, 128], "uint8"),
    "eq": ("sbuf", [128, 512], F8), "eqs": ("sbuf", [128, 512], "uint8"),
    "zq": ("sbuf", [128, C], F8), "zqs": ("sbuf", [128, C], "uint8"),
    "EB": ("sbuf", [128, 516], "bfloat16"), "ONES": ("sbuf", [128, 2 * C], "bfloat16"),
    "pi": ("sbuf", [128, 1], "int32"), "pj": ("sbuf", [128, 1], "int32"),
    "FS": ("sbuf", [128, 2 * C + 8], "float32"), "RS": ("sbuf", [128, 2 * C + 8], "float32"),
    "inv": ("sbuf", [128, 2 * C], "bfloat16"),
    "cab": ("sbuf", [128, 2 * W16], "float32"), "tab": ("sbuf", [128, 2 * W16], "float32"),
    "iab": ("sbuf", [128, 2 * W16], "int32"), "jab": ("sbuf", [128, 2 * W16], "int32"),
    "PA": ("psum", [128, 2048], "float32"), "PB": ("psum", [128, 1024], "float32"), "PS": ("psum", [128, 1024], "float32"),
}
for _n in ("X0", "X1", "TH", "THP", "TB", "TBP", "Z", "HH"):
    SCRATCH[_n] = ("sbuf", [128, 4 * C], "bfloat16")
for _n in ("RC", "NC", "CNT"):
    SCRATCH[_n] = ("sbuf", [128, 2 * C], "float32")
for _n in ("IOTA", "J16", "t1", "CODD", "CEV", "PTa", "PTb", "PTc", "OB", "SELO", "SELA", "SELP", "SEL0", "SEL1", "SEL2",
           "POS", "BPS", "APS", "VBP", "GA", "GB", "ysb", "nrs"):
    SCRATCH[_n] = ("sbuf", [128, C], "float32")
for _n in ("SELD", "SELB", "sc", "upf", "lv", "LS"):
    SCRATCH[_n] = ("sbuf", [128, C], "bfloat16")
for _n in ("p16", "p16h", "off", "noff", "thrB", "thr2", "thr3"):
    SCRATCH[_n] = ("sbuf", [128, 1], "float32")
for _n in ("C16", "jw", "offi", "offg", "m1", "m2", "m3", "posw", "af", "dpos"):
    SCRATCH[_n] = ("sbuf", [128, W16], "float32")
for _n in ("l16", "La", "Lb", "slw", "p2u", "ow", "aw"):
    SCRATCH[_n] = ("sbuf", [128, W16], "uint16")
for _k in range(1, ROUNDS + 2):
    SCRATCH["xq%d" % _k] = ("sbuf", [128, C], F8)
    SCRATCH["xs%d" % _k] = ("sbuf", [128, C], "uint8")
for _k in range(1, ROUNDS + 1):
    SCRATCH["lq%d" % _k] = ("sbuf", [128, C], F8)
    SCRATCH["ls%d" % _k] = ("sbuf", [128, C], "uint8")
    for _n in ("abw", "lab", "lnx"):
        SCRATCH[_n + str(_k)] = ("sbuf", [128, 2 * W16], "uint16")

LOCAL = ["nx", "x", "u", "ws", "wc", "v", "y0", "y1", "nr", "oc0", "oc1", "osc0", "osc1", "osc2", "osc3"]
REMOTE = ["nx", "nx2", "nx3", "ab1", "ab2", "ab3"] + [n + str(k) + str(c) for k in (1, 2, 3) for n in "qs" for c in (0, 1)]
SEMAPHORES = ["cv", "cs", "ct", "cg"] + ["d_" + n for n in LOCAL] + ["r_" + n for n in REMOTE] + ["l_" + n for n in REMOTE]


def rank_program(g, core, T, topo):
    rank = T.rank_of(core)
    if rank is None:
        return
    A = AluOpType
    AF = ActivationFunctionType
    eng = {"v": g.vector, "s": g.scalar, "t": g.tensor, "g": g, "y": g.sync}
    total, know = {}, {q: {} for q in eng}
    writes, reads = {}, {}

    def norm(k):
        return k if isinstance(k, tuple) else (k, 0, 1 << 20)

    def conflicts(table, k):
        return [e for e in table.get(k[0], []) if e[0] < k[2] and k[1] < e[1]]

    def order(q, rd, wr):
        need = []
        for k in rd:
            need += [e[2] for e in conflicts(writes, k)]
            if k[0] in ("PA", "PB", "PS"):
                need += [e[2] for e in conflicts(reads, k) if e[2][3] != q]
        for k in wr:
            need += [e[2] for e in conflicts(writes, k)]
            need += [e[2] for e in conflicts(reads, k)]
        kn = know[q]
        want = {}
        for sem, val, clock, _ in need:
            if kn.get(sem, 0) < val and want.get(sem, (0,))[0] < val:
                want[sem] = (val, clock)
        for sem in list(want):
            if any(o != sem and want[o][1].get(sem, 0) >= want[sem][0] for o in want):
                del want[sem]
        for sem, (val, clock) in want.items():
            eng[q].wait_ge(T.sem[sem], val)
            for s2, v2 in clock.items():
                kn[s2] = max(kn.get(s2, 0), v2)
            kn[sem] = max(kn.get(sem, 0), val)

    def note(q, sem, inc, rd, wr):
        total[sem] = total.get(sem, 0) + inc
        clock = dict(know[q])
        clock[sem] = total[sem]
        ev = (sem, total[sem], clock, q)
        for k in wr:
            for t in (writes, reads):
                t[k[0]] = [e for e in t.get(k[0], []) if not (k[1] <= e[0] and e[1] <= k[2])]
            writes[k[0]].append((k[1], k[2], ev))
        for k in rd:
            reads[k[0]] = reads.get(k[0], []) + [(k[1], k[2], ev)]

    COUNT = {"v": "cv", "s": "cs", "t": "ct", "g": "cg"}

    def op(q, call, rd, wr):
        rd, wr = [norm(k) for k in rd], [norm(k) for k in wr]
        order(q, rd, wr)
        call().then_inc(T.sem[COUNT[q]], 1)
        note(q, COUNT[q], 1, rd, wr)

    def dma(q, name, out, in_, rd, wr):
        rd, wr = [norm(k) for k in rd], [norm(k) for k in wr]
        order(q, rd, wr)
        eng[q].dma_start(out, in_).then_inc(T.sem["d_" + name], 16)
        note(q, "d_" + name, 16, rd, wr)

    def send(name, dst, out, in_, rd):
        order("g", [norm(rd)], [])
        rid, pid = topo.addr(dst)[:2]
        g.remote_dma(out, in_, T.sem["r_" + name], T.sem["l_" + name], pid, rid, topo.mask(core, dst))
        note("g", "l_" + name, len(topo.engines(core, dst)), [norm(rd)], [])

    def arrives(name, src, buf, lo=0, hi=1 << 20):
        n = len(topo.engines(src, core))
        total["r_" + name] = n
        writes[buf] = writes.get(buf, []) + [(lo, hi, ("r_" + name, n, {"r_" + name: n}, "x"))]

    partner = [T.cores[rank ^ m] for m in MASKS]
    for k in (1, 2, 3):
        for c, (lo, hi) in enumerate(CH):
            arrives("q%d%d" % (k, c), partner[k - 1], "lq%d" % k, lo, hi)
            arrives("s%d%d" % (k, c), partner[k - 1], "ls%d" % k, lo, hi)
        arrives("ab%d" % k, partner[k - 1], "lab%d" % k)
    arrives("nx", partner[0], "lnxi")
    for k in (2, 3):
        arrives("nx%d" % k, partner[k - 1], "lnx%d" % k)

    V, S = g.vector, g.scalar

    def ts(out, in0, s1, s2, o0, o1, rd, wr):
        if o1 is None:
            op("v", lambda: V.tensor_scalar(out, in0, s1, None, o0), rd, wr)
        else:
            op("v", lambda: V.tensor_scalar(out, in0, s1, s2, o0, o1), rd, wr)

    def tt(out, in0, in1, o, rd, wr):
        op("v", lambda: V.tensor_tensor(out, in0, in1, o), rd, wr)

    def vcopy(out, in_, rd, wr):
        op("v", lambda: V.tensor_copy(out, in_), rd, wr)

    def fill(ap, val, wr):
        op("v", lambda: V.memset(ap, val), [], wr)

    def scan(out, d0, d1, init, o0, o1, rd, wr):
        op("v", lambda: V.tensor_tensor_scan(out, d0, d1, init, o0, o1), rd, wr)

    def keep16(out, src, rd, wr):
        n = out.shape[1]
        scan(out, T.SELD[:, 0:n], src, 0.0, A.add, A.max, ["SELD"] + rd, wr)

    def act(out, in_, rd, wr, scale=None):
        if scale is None:
            op("s", lambda: S.activation(out, in_, AF.Copy), rd, wr)
        else:
            op("s", lambda: S.activation(out, in_, AF.Copy, scale=scale), rd, wr)

    def sid(out, in_, rd, wr, scale, bias):
        op("s", lambda: S.activation(out, in_, AF.Identity, bias=bias, scale=scale), rd, wr)

    def quant(codes, plane, lo, hi, src, rd):
        op("v", lambda: V.quantize_mx(T[codes][:, lo:hi], T[plane][:, lo:hi], src), rd, [(codes, lo, hi), (plane, lo, hi)])

    def mm(P, s, n, l, ls, a, r, rs, lo, hi):
        op("t", lambda: g.tensor.matmul_mx(T[P][:, 512 * s:512 * s + n], T[l][:, a:a + 128], T[ls][:, a:a + 128],
                                           T[r][:, lo:hi], T[rs][:, lo:hi], True, True),
           [(l, a, a + 128), (ls, a, a + 128), (r, lo, hi), (rs, lo, hi)], [(P, 512 * s, 512 * s + 512)])

    def bank(P, s, n):
        return T[P][:, 512 * s:512 * s + n], (P, 512 * s, 512 * s + 512)

    dma("y", "nx", T.nxi[:], T.nx[:], [], ["nxi"])
    dma("s", "x", T.X0[:], T.x[:], [], ["X0"])
    dma("y", "u", T.ut[:], T.u[:], [], ["ut"])
    dma("y", "ws", T.wsq[:], T.ws[:], [], ["wsq"])
    dma("y", "wc", T.wq[:].bitcast(dt.uint8), T.wc[:], [], ["wq"])
    dma("y", "v", T.vt[:], T.v[:], [], ["vt"])

    def iota(name, pattern):
        op("g", lambda: g.iota(T[name][:], pattern, 0, 0, allow_small_or_imprecise_dtypes=True), [], [name])

    op("g", lambda: g.iota(T.pi[:], [[0, 1]], 0, 1), [], ["pi"])
    iota("J16", [[0, W16], [1, 16]])
    iota("IOTA", [[1, C]])
    iota("C16", [[16, W16]])
    send("nx", partner[0], T.lnxi[:], T.nxi[:], "nxi")

    ts(T.pj[:], T.pi[:], 15, None, A.bitwise_and, None, ["pi"], ["pj"])
    fill(T.ONES[:], 1.0, ["ONES"])
    ts(T.p16h[:], T.pj[:], 0.5, None, A.add, None, ["pj"], ["p16h"])
    ts(T.p16[:], T.pj[:], 0.0, None, A.add, None, ["pj"], ["p16"])
    ts(T.t1[:], T.J16[:], T.p16h[:, 0:1], 2.0 ** 26, A.subtract, A.mult, ["J16", "p16h"], ["t1"])
    ts(T.off[:], T.p16[:], -K, 15.0 * K, A.mult, A.add, ["p16"], ["off"])
    ts(T.SELD[:], T.t1[:], K, None, A.min, None, ["t1"], ["SELD"])
    vcopy(T.La[:], T.nxi[:], ["nxi"], ["La"])
    fill(T.ow[:], 0, ["ow"])
    fill(T.OB[:, 0:1], 0.0, [("OB", 0, 1)])
    op("g", lambda: g.affine_select(T.EB[:], T.ONES[:, 0:516], [[1, 516]], A.is_equal, 0.0, -4, -4), ["ONES"], ["EB"])

    def table(i):
        if i == 1:
            sid(T.jw[:], T.C16[:], ["C16", "p16"], ["jw"], 1.0, T.p16[:, 0:1])
            sid(T.offi[:], T.jw[:], ["jw", "off"], ["offi"], 1024.0, T.off[:, 0:1])
        if i == 2:
            sid(T.CODD[:], T.IOTA[:], ["IOTA"], ["CODD"], 1024.0, 512.0)
        if i == 3:
            act(T.CEV[:], T.IOTA[:], ["IOTA"], ["CEV"], scale=1024.0)
        if i == 4:
            sid(T.offg[:], T.offi[:], ["offi"], ["offg"], 1.0, 512.0)
            sid(T.noff[:], T.off[:], ["off"], ["noff"], -1.0, 0.0)
        if i == 7:
            sid(T.thrB[:], T.off[:], ["off"], ["thrB"], 2.0 ** -19, 0.5)
            sid(T.thr2[:], T.off[:], ["off"], ["thr2"], 1.0, 400000.0)
            sid(T.thr3[:], T.off[:], ["off"], ["thr3"], 1.0, -600000.0)
            sid(T.FS[:, 0:1], T.p16[:], ["p16"], [("FS", 0, 1)], 0.0, -float(2 ** 20))
            sid(T.RS[:, 2 * C + 7:2 * C + 8], T.p16[:], ["p16"], [("RS", 2 * C + 7, 2 * C + 8)], 0.0, float(2 ** 19))

    def ucols():
        vcopy(T.l16[:], T.C16[:], ["C16"], ["l16"])
        quant("uq", "uqs", 0, 128, T.ut[:], ["ut"])
        vcopy(T.up16[:, 0:128].bitcast(dt.uint32), T.uq[:, 0:128].bitcast(dt.uint32).indirect(T.l16[:, 0:8]), ["uq", "l16"], ["up16"])
        act(T.up16s[:, 0:128], T.uqs[:, 0:128].indirect(T.l16[:, 0:8]), ["uqs", "l16"], ["up16s"])

    def etiles():
        for b in range(4):
            quant("eq", "eqs", 128 * b, 128 * b + 128, T.EB[:, 4 - b:516 - b], ["EB"])

    def scores(k, c):
        lo, hi = CH[c]
        mm("PS", c, hi - lo, "up16", "up16s", 0, "xq%d" % k, "xs%d" % k, lo, hi)

    def ship(k, c):
        p, (lo, hi) = partner[k - 1], CH[c]
        send("q%d%d" % (k, c), p, T["lq%d" % k][:, lo:hi].bitcast(dt.uint8), T["xq%d" % k][:, lo:hi].bitcast(dt.uint8), ("xq%d" % k, lo, hi))
        send("s%d%d" % (k, c), p, T["ls%d" % k][:, lo:hi], T["xs%d" % k][:, lo:hi], ("xs%d" % k, lo, hi))

    def signs():
        for c, (lo, hi) in enumerate(CH):
            src, key = bank("PS", c, hi - lo)
            op("s", lambda: S.activation(T.sc[:, lo:hi], src, AF.Sign), [key], [("sc", lo, hi)])
            ts(T.upf[:, lo:hi], T.sc[:, lo:hi], 0.0, None, A.max, None, [("sc", lo, hi)], [("upf", lo, hi)])

    def unpack(k):
        for b in range(4):
            mm("PA", b, C, "eq", "eqs", 128 * b, "xq%d" % k, "xs%d" % k, 0, C)

    def keep(b):
        src, key = bank("PA", b, C)
        act(T.TH[:, C * b:C * b + C], src, [key], [("TH", C * b, C * b + C)], scale=0.5)

    def unpack_far(k, b):
        src, key = bank("PB", b % 2, C)
        mm("PB", b % 2, C, "eq", "eqs", 128 * b, "lq%d" % k, "ls%d" % k, 0, C)
        act(T.THP[:, C * b:C * b + C], src, [key], [("THP", C * b, C * b + C)], scale=0.5)

    def places():
        keep16(T.SELP[:], T.POS[:], ["POS"], ["SELP"])
        sid(T.posw[:], T.SELP[:, 15:C:16], ["SELP", "noff"], ["posw"], 1.0, T.noff[:, 0:1])

    def lay_order():
        ts(T.p2u[:], T.SELP[:, 15:C:16], T.off[:, 0:1], 2.0 ** -10, A.subtract, A.mult, ["SELP", "off"], ["p2u"])
        op("v", lambda: V.tensor_copy(T.OB[:].indirect(T.p2u[:]), T.IOTA[:]), ["IOTA", "p2u"], ["OB"])

    def far_ring(lst, key):
        act(T.APS[:], T.IOTA[:].indirect(T[lst][:, 0:W16]), ["IOTA", key], ["APS"])

    def far_places(lst):
        sid(T.VBP[:], T.POS[:].indirect(T[lst][:, W16:2 * W16]), ["POS", lst], ["VBP"], 1.0, 512.0)

    def guests(lo, hi):
        tt(T.RC[:, 1 + 2 * lo:2 * hi:2], T.APS[:].indirect(T.ow[:, lo // 16:hi // 16]), T.CODD[:, lo:hi], A.add,
           ["APS", ("ow", lo, hi), "CODD"], [("RCO", lo, hi)])

    def evens(lo, hi):
        tt(T.RC[:, 2 * lo:2 * hi:2], T.OB[:, lo:hi], T.CEV[:, lo:hi], A.add, [("OB", lo, hi), "CEV"], [("RCE", lo, hi)])

    def guest_scan(lo, hi):
        keep16(T.SELA[:, lo:hi], T.RC[:, 1 + 2 * lo:2 * hi:2], [("RCO", lo, hi)], [("SELA", lo, hi)])

    def guest_cols():
        tt(T.af[:], T.SELA[:, 15:C:16], T.offg[:], A.subtract, ["SELA", "offg"], ["af"])

    def guest_list():
        vcopy(T.aw[:], T.af[:], ["af"], ["aw"])

    def hosts():
        keep16(T.SEL0[:], T.VBP[:], ["VBP"], ["SEL0"])
        tt(T.dpos[:], T.SEL0[:, 15:C:16], T.SELP[:, 15:C:16], A.subtract, ["SEL0", "SELP"], ["dpos"])

    def negatives():
        sid(T.NC[:], T.RC[:], ["RCE", "RCO"], ["NC"], 1.0, -float(2 ** 19))

    def leavers(lst):
        tt(T.lv[:], T.upf[:].indirect(T[lst][:, W16:2 * W16]), T.sc[:], A.is_lt, ["upf", "sc", lst], ["lv"])

    def void_evens():
        act(T.inv[:, 0:2 * C:2], T.lv[:].indirect(T.ow[:]), ["lv", "ow"], ["inve"])

    def leaver_bits():
        scan(T.LS[:], T.SELB[:], T.lv[:], 0.0, A.add, A.max, ["SELB", "lv"], ["LS"])

    def splice(k):
        lst, abw = "lnx%d" % k, "abw%d" % k
        h = W16
        if k > 1:
            leavers(lst)
            keep(0)
            keep(1)
            void_evens()
        sid(T.inv[:, 1 + 2 * GS:2 * C:2], T.lv[:].indirect(T.aw[:, GS // 16:h]), ["lv", "aw"], ["invp"], -1.0, 1.0)
        if k > 1:
            leaver_bits()
        ts(T.inv[:, 1:2 * GS:2], T.lv[:].indirect(T.aw[:, 0:GS // 16]), -1.0, 1.0, A.mult, A.add, ["lv", "aw"], ["invo"])
        ts(T.m1[:], T.LS[:, 15:C:16], T.thrB[:, 0:1], None, A.is_ge, None, ["LS", "thrB"], ["m1"])
        tt(T.m2[:], T.m1[:], T.dpos[:], A.mult, ["m1", "dpos"], ["m2"])
        tt(T.m3[:], T.m2[:], T.posw[:], A.add, ["m2", "posw"], ["m3"])
        ts(T.slw[:], T.m3[:], 2.0 ** -9, None, A.mult, None, ["m3"], ["slw"])
        keep(2)
        keep(3)
        void = ["inve", "invo", "invp"]
        scan(T.FS[:, 1:2 * C + 1], T.inv[:], T.NC[:], -float(2 ** 20), A.mult, A.min, void + ["NC"], [("FS", 1, 2 * C + 8)])
        act(T.GB[:], T.FS[:, 0:2 * C].indirect(T.slw[:]), ["FS", "slw"], ["GB"])
        scan(T.RS[:, 2 * C + 6:6:-1], T.inv[:, ::-1], T.RC[:, ::-1], float(2 ** 19), A.mult, A.max,
             void + ["RCE", "RCO"], [("RS", 0, 2 * C + 7)])
        act(T.GA[:], T.RS[:, 8:2 * C + 8].indirect(T.slw[:]), ["RS", "slw"], ["GA"])
        keep16(T.SEL1[:], T.GB[:], ["GB"], ["SEL1"])
        sid(T.cab[:, h:2 * h], T.SEL1[:, 15:C:16], ["SEL1", "noff"], [("cab", h, 2 * h)], 1.0, T.noff[:, 0:1])
        if k < ROUNDS:
            scan(T.CNT[:, 0:C], T.ONES[:, 0:C], T.inv[:, 0:C], -1.0, A.add, A.subtract, ["ONES"] + void, [("CNT", 0, C)])
        else:
            quant("vq", "vqs", 0, 128, T.vt[:], ["vt"])
        keep16(T.SEL2[:], T.GA[:], ["GA"], ["SEL2"])
        sid(T.cab[:, 0:h], T.SEL2[:, 15:C:16], ["SEL2", "noff"], [("cab", 0, h)], 1.0, T.noff[:, 0:1])
        ts(T.tab[:, h:2 * h], T.SEL1[:, 15:C:16], T.thr3[:, 0:1], T.FS[:, 2 * C:2 * C + 1], A.is_le, A.mult, ["SEL1", "thr3", "FS"], [("tab", h, 2 * h)])
        ts(T.tab[:, 0:h], T.SEL2[:, 15:C:16], T.thr2[:, 0:1], T.RS[:, 7:8], A.is_ge, A.mult, ["SEL2", "thr2", "RS"], [("tab", 0, h)])
        tt(T.iab[:], T.cab[:], T.tab[:], A.add, ["cab", "tab"], ["iab"])
        ts(T.jab[:], T.iab[:], 511, None, A.bitwise_and, None, ["iab"], ["jab"])
        vcopy(T[abw][:], T.jab[:], ["jab"], [abw])
        send("ab%d" % k, partner[k - 1], T["lab%d" % k][:], T[abw][:], abw)
        if k < ROUNDS:
            send("nx%d" % (k + 1), partner[k], T["lnx%d" % (k + 1)][:], T[abw][:], abw)

    def jump(out, win, lst, share):
        for lo, hi in CH0[::-1] if share else CH0:
            (vcopy if share and lo == 0 else act)(T[out][:, lo:hi], T[win][:].indirect(T[lst][:, lo // 16:hi // 16]), [win, lst], [(out, lo, hi)])

    def ahead(P, m, n, a):
        b = 0 if m < 16 else m
        act(T.OB[:, m:m + n], T[P][:].indirect(T.ow[:, a // 16:(a + n) // 16]), [P, ("ow", a, a + n)], [("OB", m, m + n)])
        keep16(T.SELO[:, b:b + n], T.OB[:, b:b + n], [("OB", b, b + n)], [("SELO", b, b + n)])

    def enlist(m, n):
        b = 0 if m < 16 else m
        ts(T.ow[:, b // 16:(b + n) // 16], T.SELO[:, b + 15:b + n:16], T.off[:, 0:1], None, A.subtract, None,
           [("SELO", b, b + n), "off"], [("ow", b, b + n)])

    jump("PTa", "IOTA", "La", True)
    for i in range(TOP + 1):
        L, L2 = ("La", "Lb") if i % 2 == 0 else ("Lb", "La")
        P, P2 = (("PTa", "PTb"), ("PTb", "PTc"), ("PTc", "PTa"))[i % 3]
        n = "SEL%d" % (i % 3)
        if i < TOP:
            jump(P2, P, L, i < 3)
        if i < TOP - 1:
            for lo, hi in CH0:
                keep16(T[n][:, lo:hi], T[P2][:, lo:hi], [(P2, lo, hi)], [(n, lo, hi)])
        ahead(P, 2 ** i, max(16, 2 ** i), 0)
        if i < TOP - 1:
            ts(T[L2][:], T[n][:, 15:C:16], T.off[:, 0:1], None, A.subtract, None, [n, "off"], [L2])
        enlist(2 ** i, max(16, 2 ** i))
        table(i)
        if i == 1:
            ucols()
        if i == 2:
            etiles()
        if i == 3:
            for c, (lo, hi) in enumerate(CH):
                quant("xq1", "xs1", lo, hi, T.X0[:, 4 * lo:4 * hi], ["X0"])
                scores(1, c)
                ship(1, c)
            unpack(1)
        if i == 4:
            vcopy(T.lnx1[:, 0:W16], T.lnxi[:], ["lnxi"], [("lnx1", 0, W16)])
            op("v", lambda: V.tensor_copy(T.BPS[:].indirect(T.lnx1[:, 0:W16]), T.IOTA[:]), ["IOTA", ("lnx1", 0, W16)], ["BPS"])
        if i == 5:
            far_ring("lnx1", ("lnx1", 0, W16))
            signs()
            keep16(T.SELA[:], T.BPS[:], ["BPS"], ["SELA"])
            ts(T.lnx1[:, W16:2 * W16], T.SELA[:, 15:C:16], T.off[:, 0:1], None, A.subtract, None, ["SELA", "off"], [("lnx1", W16, 2 * W16)])
    far = ("PTa", "PTb", "PTc")[TOP % 3]
    leavers("lnx1")
    ahead(far, 128, 64, 64)
    enlist(128, 64)
    guests(0, 128)
    act(T.SELB[:], T.SELD[:], ["SELD"], ["SELB"], scale=2.0 ** -19)
    ahead(far, 192, 64, 128)
    enlist(192, 64)
    guest_scan(0, 128)
    keep(0)
    leaver_bits()
    ahead(far, 256, 64, 192)
    enlist(256, 64)
    evens(0, 192)
    ahead(far, 320, 32, 256)
    enlist(320, 32)
    guests(128, C)
    op("v", lambda: V.tensor_copy(T.POS[:].indirect(T.ow[:]), T.CEV[:]), ["ow", "CEV"], ["POS"])
    void_evens()
    table(7)
    keep(1)
    far_places("lnx1")
    guest_scan(128, C)
    places()
    guest_cols()
    evens(192, C)
    guest_list()
    negatives()
    hosts()

    for k in range(1, ROUNDS + 1):
        last = k == ROUNDS
        if k > 1:
            signs()
        splice(k)
        abw, lab, lnx = "abw%d" % k, "lab%d" % k, "lnx%d" % (k + 1)
        xq, xs = "xq%d" % (k + 1), "xs%d" % (k + 1)

        def own(t, q, lo=0, hi=C):
            (act if q == "s" else vcopy)(T.TB[:, C * t + lo:C * t + hi],
                                         T.TH[:, C * t:C * t + C].indirect(T[abw][:, W16 + lo // 16:W16 + hi // 16]),
                                         [("TH", C * t, C * t + C), abw], [("TB", C * t + lo, C * t + hi)])
        if not last:
            scan(T.CNT[:, C:2 * C], T.ONES[:, C:2 * C], T.inv[:, C:2 * C], T.CNT[:, C - 1:C], A.add, A.subtract,
                 ["ONES", "inve", "invo", "invp", ("CNT", 0, C)], [("CNT", C, 2 * C)])
            unpack_far(k, 0)
            act(T.POS[:], T.CNT[:].indirect(T.slw[:]), ["CNT", "slw"], ["POS"], scale=1024.0)
            own(0, "v")
            for b in (1, 2, 3):
                unpack_far(k, b)
            places()
            own(1, "s")
            lay_order()
            keep16(T.SELO[:], T.OB[:], ["OB"], ["SELO"])
            evens(0, C)
            ts(T.ow[:], T.SELO[:, 15:C:16], T.off[:, 0:1], None, A.subtract, None, ["SELO", "off"], ["ow"])
        else:
            for b in range(4):
                unpack_far(k, b)
            for t in range(4):
                own(t, "v")
        for c, (lo, hi) in enumerate(CH):
            for t in range(4):
                W = C * t
                act(T.TBP[:, W + lo:W + hi], T.THP[:, W:W + C].indirect(T[lab][:, W16 + lo // 16:W16 + hi // 16]),
                    [("THP", W, W + C), lab], [("TBP", W + lo, W + hi)])
                tt(T.Z[:, 4 * lo + t:4 * hi:4], T.THP[:, W:W + C].indirect(T[lab][:, lo // 16:hi // 16]), T.TBP[:, W + lo:W + hi], A.add,
                   [("THP", W, W + C), lab, ("TBP", W + lo, W + hi)], [("Z%d" % t, lo, hi)])
            quant("zq", "zqs", lo, hi, T.Z[:, 4 * lo:4 * hi], [("Z%d" % t, lo, hi) for t in range(4)])
        if not last:
            far_ring(lnx, lnx)
        else:
            act(T.nrs[:], T.IOTA[:].indirect(T[abw][:, 0:W16]), ["IOTA", abw], ["nrs"])
            dma("y", "nr", T.nr[:], T.nrs[0:128:16, :], ["nrs"], [])
        for c, (lo, hi) in enumerate(CH):
            for b in range(4):
                P, s = ("PA", b) if c == 0 else ("PB", b) if b < 2 else ("PA", b - 2)
                mm(P, s, hi - lo, "wq", "wsq", 128 * b, "zq", "zqs", lo, hi)
                src, key = bank(P, s, hi - lo)
                if last and c == 1 and b % 2:
                    ts(T.HH[:, C * b + lo:C * b + hi], src, 2.0 ** -6, None, A.mult, None, [key], [("HH", C * b + lo, C * b + hi)])
                else:
                    act(T.HH[:, C * b + lo:C * b + hi], src, [key], [("HH", C * b + lo, C * b + hi)], scale=2.0 ** -6)
        if not last:
            guests(0, C)
            guest_scan(0, C)
            guest_cols()
            for lo, hi in CH:
                for t in (2, 3):
                    own(t, "s", lo, hi)
            far_places(lnx)
            negatives()
        for c, (lo, hi) in enumerate(CH):
            for t in range(4):
                W = C * t
                tt(T.X1[:, 4 * lo + t:4 * hi:4], T.HH[:, W:W + C].indirect(T[abw][:, lo // 16:hi // 16]), T.TB[:, W + lo:W + hi], A.add,
                   [("HH", W, W + C), abw, ("TB", W + lo, W + hi)], [("X1_%d" % t, lo, hi)])
                if not last and c == 0 and t == 0:
                    guest_list()
            quant(xq, xs, lo, hi, T.X1[:, 4 * lo:4 * hi], [("X1_%d" % t, lo, hi) for t in range(4)])
            if not last:
                scores(k + 1, c)
                ship(k + 1, c)
            else:
                mm("PS", c, hi - lo, "vq", "vqs", 0, xq, xs, lo, hi)
                dma("y", "oc%d" % c, T.oc[:, 4 * lo:4 * hi], T[xq][:, lo:hi].bitcast(dt.uint8), [(xq, lo, hi)], [])
                if c == 1:
                    for i in range(4):
                        dma("y", "osc%d" % i, T.osc[4 * i:4 * i + 4, :], T[xs][32 * i:32 * i + 4, :], [xs], [])
                src, key = bank("PS", c, hi - lo)
                act(T.ysb[:, lo:hi], src, [key], [("ysb", lo, hi)])
                dma("y", "y%d" % c, T.y[:, lo:hi], T.ysb[:, lo:hi], [("ysb", lo, hi)], [])
        if not last:
            unpack(k + 1)
            hosts()
    for sem, val in total.items():
        if know["g"].get(sem, 0) < val:
            g.wait_ge(T.sem[sem], val)
